import numpy as np, ml_dtypes
CORES = [6,15,38,47]
N = 4
BF = ml_dtypes.bfloat16
def gentries(a):
    return np.ascontiguousarray(a.reshape(8, 16, -1).transpose(0, 2, 1)).reshape(8, -1)
def gtable(e):
    e = np.asarray(e); return np.ascontiguousarray(e.reshape(8, -1, 16).transpose(0, 2, 1)).reshape(128, -1).astype(np.int32)
W, V, Q, L, B, RO = 3840, 1024, 4, 256, 4, 6
def parts(rng):
    x = rng.integers(0, 16, (N, 8, 16, W)); s = rng.integers(0, 256, (N, 8, 16, W))
    p = rng.integers(0, W, (N, 8, 16, V)); u = rng.integers(0, V, (N, 8, 16, V))
    share = rng.choice(np.array([0.0006, 0.0025, 0.008, 0.025]), (N, 8, 1, 1))
    m = np.where(rng.random((N, 8, 16, V)) < share, rng.integers(8, 16, (N, 8, 16, V)), rng.integers(0, 8, (N, 8, 16, V)))
    h = np.ascontiguousarray(np.argsort(rng.random((N, 8, V)), axis=-1)[..., :B * L])
    c = rng.integers(132, 157, (N, 8, 1)) + rng.integers(0, 8, (N, 8, 16)); t = rng.integers(45, 111, (N, 8, 16, RO))
    return x, s, p, u, m, h, c, t
def pack(x, s, p, u, m, h, c, t):
    def w(a): return np.ascontiguousarray(a.reshape(N, 128, -1))
    return {"xf": w(x).astype(np.float32).astype(BF), "stp": w(s).astype(np.float32).astype(BF), "pl": w(p).astype(np.int32), "su": w(u).astype(np.int32),
            "mk": w(m).astype(np.float32).astype(BF), "hp": np.stack([gtable(a) for a in h]), "cp": w(c).astype(np.int32), "th": w(t).astype(np.int32)}
def setup_inputs(rng):
    return pack(*parts(rng))
def uneven(rng, n, k, e):
    return np.minimum((n * rng.random((N, 8, 16, k)) ** np.exp2(e)).astype(np.int64), n - 1)
def setup_inputs_spread(rng):
    x, s, p, u, m, h, c, t = parts(rng)
    x = uneven(rng, 16, W, rng.integers(-2, 3, (N, 8, 1, W))); s = uneven(rng, 256, W, rng.integers(-2, 3, (N, 8, 1, W)))
    p = uneven(rng, W, V, rng.integers(-2, 3, (N, 8, 1, 1))); u = uneven(rng, V, V, rng.integers(-2, 3, (N, 8, 1, 1)))
    m = np.where(rng.random((N, 8, 16, V)) < rng.choice(np.array([0.0, 0.0, 0.0, 0.0, 0.01, 0.05]), (N, 8, 1, V)), rng.integers(0, 16, (N, 8, 16, V)), 0)
    c = rng.integers(0, 241, (N, 8, 16)); t = rng.integers(1, 241, (N, 8, 16, RO))
    c[:, 1::2] = rng.integers(100, 241, (N, 4, 16)); t[:, 1::2] = rng.integers(100, 241, (N, 4, 16, RO))
    return pack(x, s, p, u, m, h, c, t)
def binary(rng, n):
    k = rng.integers(0, 3, (N, 8, 1, n)); return np.where(k == 2, rng.integers(0, 2, (N, 8, 16, n)), k)
def setup_inputs_ends(rng):
    x, s, p, u, m, h, c, t = parts(rng)
    x = 15 * binary(rng, W); s = 255 * binary(rng, W)
    x[..., 0] = 0; x[..., 1] = 15; x[..., 2] = 15; x[..., W - 1] = 15; x[:, 1:6:2, :, 0] = 15 * rng.integers(0, 2, (N, 3, 16))
    s[..., W - 1] = 255 * rng.integers(0, 2, (N, 8, 16)); s[..., 0] = 255 * rng.integers(0, 2, (N, 8, 16))
    k = rng.integers(0, 10, (N, 8, 1, V)); z = rng.random((N, 8, 16, V))
    p = np.where(k < 2, 0, np.where(k < 4, W - 1, np.where(z < 0.35, 0, np.where(z < 0.7, W - 1, p))))
    p[..., 0] = 0; p[..., V - Q:] = W - 1
    k = rng.integers(0, 10, (N, 8, 1, V)); z = rng.random((N, 8, 16, V))
    u = np.where(k < 4, 0, np.where(k < 6, V - 1, np.where(z < 0.25, 0, np.where(z < 0.5, V - 1, u))))
    m = 15 * ((rng.random((N, 8, 1, V)) < 0.03) | (rng.random((N, 8, 16, V)) < 0.004)).astype(np.int64)
    m[..., 0] = 0; m[..., V - 1] = 15 * rng.integers(0, 2, (N, 8, 16)); m[N - 1, 7, :, V - 1] = 15
    e = np.stack([np.arange(V // 2), V - 1 - np.arange(V // 2)], axis=1).reshape(-1)[:B * L]
    h[:, (0, 2, 6)] = e; h[:, (1, 3, 7)] = e[::-1]
    k = np.stack([rng.permutation(np.array([0, 0, 0, 1, 1, 2, 2, 2])) for r in range(N)])[:, :, None]
    c = 240 * np.where(k == 2, rng.integers(0, 2, (N, 8, 16)), k); c[N - 1, 7] = 0
    t = np.where(rng.random((N, 8, 16, RO)) < 0.25, 1, 240)
    return pack(x, s, p, u, m, h, c, t)
def setup_inputs_corners(rng):
    x, s, p, u, m, h, c, t = parts(rng)
    near = rng.random((N, 8, 16, V)) < 0.25; p = np.where(near, W - 1 - rng.integers(0, 256, (N, 8, 16, V)), p)
    a = W - np.arange(W - 255, W); s[..., W - 255:] = np.minimum(a + rng.integers(-1, 2, (N, 8, 16, 255)), 255)
    x[:, ::2] = 7 + (np.arange(W) & 1)
    odd = (rng.random((N, 4, 16, V)) < rng.random((N, 4, 1, V))).astype(np.int64); p[:, ::2] = (p[:, ::2] >> 1) * 2 + odd
    c[:, ::2] = 112 + rng.integers(4, 13, (N, 4, 16)); t[:, ::2] = rng.integers(7, 9, (N, 4, 16, RO)) * rng.integers(6, 17, (N, 4, 16, RO)) + rng.integers(0, 2, (N, 4, 16, RO))
    m = rng.choice(np.array([0, 3, 4, 7, 8, 11, 12, 15]), (N, 8, 16, V), p=np.array([0.3, 0.15, 0.15, 0.308, 0.04, 0.05, 0.001, 0.001]))
    v = np.arange(V)
    for r in range(N):
        o = rng.permutation(8)
        m[r, o[0]] = 15; m[r, o[1]] = 0
        m[r, o[2]] = np.where(rng.random((16, V)) < 0.002, rng.integers(11, 13, (16, V)), 7)
        o = rng.permutation(8)
        u[r, o[0]] = v; u[r, o[1]] = (v + V - 1) % V; u[r, o[2]] = rng.choice(np.array([0, V - 1]), (16, V)); u[r, o[3]] = (v + 1) % V
        p[r, o[4]] = p[r, o[4], :1]
    return pack(x, s, p, u, m, h, c, t)
def setup_inputs_crowd(rng):
    x, s, p, u, m, h, c, t = parts(rng)
    for r in range(N):
        o = rng.permutation(8)
        for i in range(6):
            g = o[i]; lone = Q * int(rng.choice(np.array([0, L // 2, L - 1]))) + np.arange(Q)
            w = rng.permutation(np.setdiff1d(np.arange(V), lone)); hot = w[:16]
            m[r, g] = 0
            if i < 4: c[r, g] = 240
            if i in (0, 1, 3): m[r, g, np.arange(16), hot] = 15
            if i < 2: u[r, g] = hot[:, None]
            if i == 1: u[r, g][:, lone] = lone
            if i == 2: u[r, g] = V - 1
            if i == 3: u[r, g] = w[16]; u[r, g][:, lone] = hot[:, None]
            if i >= 4:
                p[r, g] = W - 1; x[r, g, :, W - 1] = 15; x[r, g, :, 0] = 0
                c[r, g] = rng.integers(229, 237, 16); t[r, g] = rng.integers(1, 121, (16, RO)); u[r, g] = V - 1
            if i == 5: p[r, g][:, lone] = 0; u[r, g] = np.arange(V)
    return pack(x, s, p, u, m, h, c, t)
def setup_inputs_tides(rng):
    x, s, p, u, m, h, c, t = parts(rng); x = np.minimum(x, 14); q = rng.permutation(N); a, b, e = int(q[0]), int(q[1]), int(q[2]); v = np.arange(V)
    for g in range(8):
        o = rng.permutation(16)[:RO]
        m[:, g, o] = m[:, g, o] & 7; t[:, g, o] = 240
        for r in (a, e):
            m[r, g] = m[r, g] & 7; u[r, g] = Q * rng.integers(0, L, (16, V)) + v % Q
        x[a, g] = np.maximum(x[a, g], 1); c[a, g, ::2] = rng.integers(0, 9, 8); t[a, g, o, np.arange(RO)] = rng.integers(1, 9, RO)
        k = rng.integers(0, 12, (16, V)); k[o] = k[o] & 7; m[b, g] = k
        c[b, g] = 240; t[b, g] = rng.integers(1, 241, (16, RO))
        c[e, g] = rng.integers(116, 141, 16); t[e, g] = 240
        even = np.arange(0, RO, 2); t[e, g, o[even], even] = rng.integers(24, 57, len(even))
    return pack(x, s, p, u, m, h, c, t)
def check_inputs(d):
    bad = []
    for k, lo, hi in (("xf", 0, 15), ("stp", 0, 255), ("pl", 0, W - 1), ("su", 0, V - 1), ("mk", 0, 15), ("hp", 0, V - 1), ("cp", 0, 240), ("th", 1, 240)):
        v = np.asarray(d[k]).astype(np.float64)
        if not np.all((v >= lo) & (v <= hi)): bad.append("range of " + k)
        elif not np.all(v == np.floor(v)): bad.append("whole numbers in " + k)
    e = np.sort(np.stack([gentries(a) for a in d["hp"]]), axis=-1)
    if np.any(e[..., 1:] == e[..., :-1]): bad.append("repeats in hp")
    return bad
def pick(a, ix):
    return np.stack([np.stack([np.take(a[r, g], ix[r, g], axis=1) for g in range(8)]) for r in range(N)])
def reference(xf, stp, pl, su, mk, hp, cp, th):
    x = xf.astype(np.float32).astype(np.int32).reshape(N, 8, 16, W); s = stp.astype(np.float32).astype(np.int32).reshape(N, 8, 16, W)
    p = pl.astype(np.int32).reshape(N, 8, 16, V); nx = su.astype(np.int32).reshape(N, 8, 16, V); m = mk.astype(np.float32).astype(np.int32).reshape(N, 8, 16, V)
    h = np.stack([gentries(a) for a in hp]).astype(np.int32).reshape(N, 8, B, L); cap = cp.astype(np.int32).reshape(N, 8, 16, 1); theta = th.astype(np.int32).reshape(N, 8, 16, RO)
    wt = (2 * np.arange(16, dtype=np.int32) + 1).reshape(1, 1, 16, 1); A = np.zeros((N, 8, 1, 1), np.int32)
    for t in range(RO):
        lanes = slice(t % Q, V, Q)
        old = m[..., lanes].copy(); at = p[..., lanes].copy()
        climb = np.max(pick(m, nx[..., lanes].reshape(N, 8, 16 * L)).reshape(N, 8, 16, 16, L), axis=3)
        new = np.maximum(old, climb - 4)
        ix = at.reshape(N, 8, 16 * L)
        xk = pick(x, ix).reshape(N, 8, 16, 16, L)
        S = np.add.reduce(xk, axis=3)
        over = S > cap + (A & 7)
        load = np.add.reduce(np.where(over[:, :, :, None, :], xk, 0), axis=2)
        new = np.where(load >= theta[..., t:t + 1], 15, new)
        opened = np.any((new >= 8) & (old < 8), axis=2)
        u = np.add.reduce(wt * S, axis=2)
        move = np.where(new >= 8, np.maximum(u & 15, 1)[:, :, None, :], 0)
        sk = pick(s, ix).reshape(N, 8, 16, 16, L)
        child = at + np.take_along_axis(sk, move[:, :, None], axis=2)[:, :, 0]
        child = np.where(child >= W, child - W, child)
        c = np.take_along_axis(h, ((u >> 4) & (B - 1))[:, :, None], axis=2)[:, :, 0]
        A = np.add.reduce(opened.astype(np.int32), axis=2).reshape(N, 8, 1, 1)
        m[..., lanes] = new
        back = np.zeros((N, 8, 16, L), np.int32)
        for r in range(N):
            d = (r + 1 + t % (N - 1)) % N
            for g in range(8):
                i = np.flatnonzero(opened[r, g]); cc = c[r, g, i]
                back[r, g][:, i] = m[d, g][:, cc]
                p[d, g][:, cc] = child[r, g][:, i]; m[d, g][:, cc] = 0
        now = m[..., lanes]
        m[..., lanes] = np.where(opened[:, :, None, :], np.maximum(now, back - 4), now)
    return {"ypl": p.reshape(N, 128, V).astype(np.float32), "ymk": m.reshape(N, 128, V).astype(np.float32).astype(BF)}

@@ -1,0 +1,514 @@
+from concourse.mybir import AluOpType as Op, ActivationFunctionType as Fn, AxisListType as Ax
+
+W, V, L, RO = 3840, 1024, 256, 6
+WX = 5120
+VX = V + L
+BF, F32, I32, U16 = "bfloat16", "float32", "int32", "uint16"
+
+
+def _sb(n, d):
+    return ("sbuf", [128, n], d)
+
+
+SCRATCH = {
+    "X": _sb(WX, BF), "ST": _sb(WX, BF), "P": _sb(VX, F32), "PL": _sb(V, I32), "IF": _sb(128, F32), "M": _sb(VX, BF),
+    "SU": _sb(V, I32), "SL": _sb(V, U16), "HP": _sb(64, I32), "CP": _sb(4, I32), "TH": _sb(8, I32),
+    "hc": _sb(64, F32), "hd": _sb(32, F32), "he": _sb(32, F32), "cpf": _sb(4, F32), "thf": _sb(8, F32), "capa": _sb(4, F32),
+    "xk": _sb(4096, BF), "sk": _sb(4096, BF), "skT": _sb(4096, BF), "gm": _sb(4096, BF), "sc": _sb(4096, BF), "y": _sb(4096, BF),
+    "seg": _sb(1536, BF), "offs": _sb(L, U16), "offs2": _sb(L, U16), "O2": _sb(64, U16),
+    "Sb": _sb(L, BF), "pre": _sb(L, BF), "thp": _sb(L, BF), "nold": _sb(L, BF), "hi": _sb(L, BF), "f15": _sb(L, BF),
+    "R": _sb(L, BF), "tt1": _sb(L, BF), "t2": _sb(L, F32), "t3": _sb(L, F32), "back": _sb(L, BF),
+    "ui": _sb(24, I32), "b0": _sb(32, I32), "b1": _sb(16, I32), "pq": _sb(32, F32), "pr": _sb(32, F32), "rr": _sb(16, F32),
+    "cc": _sb(16, F32), "jj": _sb(16, I32), "jm": _sb(16, F32), "ja": _sb(16, F32), "jl": _sb(16, U16), "jb": _sb(16, F32),
+    "tm": _sb(16, F32), "ob": _sb(16, BF), "af": _sb(4, F32), "aw": _sb(16, F32), "ak": _sb(8, BF), "dl": _sb(16, BF),
+    "NEW": _sb(RO * L, BF), "L1": _sb(RO * 16, U16), "CH": _sb(RO * L, U16),
+    "MR": _sb(RO * VX, BF), "FR": _sb(RO * L, BF), "L1R": _sb(RO * 16, U16), "CHR": _sb(RO * L, U16),
+    "ip": _sb(4, I32), "KI": _sb(8, I32), "KF": _sb(8, F32), "KD": _sb(16, F32),
+    "ion": _sb(144, BF), "iog": _sb(128, BF), "io16": _sb(16, F32),
+    "WE": _sb(144, BF), "WW": _sb(144, BF), "WS": _sb(144, BF), "WH": _sb(144, BF), "MAT": _sb(12 * 128, BF),
+    "sg": _sb(L, BF), "th2": _sb(24, F32),
+    "pS": ("psum", [128, 512], F32), "pO": ("psum", [128, 512], F32), "pL": ("psum", [128, 512], F32),
+    "pU": ("psum", [128, 512], F32), "pC": ("psum", [128, 512], F32), "pZ": ("psum", [128, 512], F32),
+    "pD": ("psum", [128, 512], F32), "pA": ("psum", [128, 512], F32),
+}
+LOADS = ["d_mk", "d_su", "d_su2", "d_pl", "d_x", "d_s", "d_xe", "d_se", "d_hp", "d_cp", "d_th", "d_om", "d_op"]
+SEMAPHORES = (["cv", "ca", "ct", "cg"] + LOADS + ["lm", "ln", "l1", "l2"]
+              + ["%s%d" % (k, t) for k in ("am", "an", "a1", "a2") for t in range(RO)])
+
+PLAN = {
+    "split": 256,
+    "main0": "SC L:0-128 ma:0-64 mv:64-128 L:128-256 ma:128-192 IC F ma:192-256 c:0-64 c:64-128 c:128-192 n SI D0 "
+             "xa:0-32 xv:32-64 xa:64-96 xv:96-128 xa:128-192 xv:192-256 S:0-64 S:64-128 S:128-192 S:192-256 "
+             "o c:192-256 PC at p h O B sa:0-64 sa:64-128 sa:128-192 sa:192-256 SD "
+             "y:0-256:0-2 U y:0-256:2-8 u:0-1 y:0-256:8-9 u:1-3 y:0-256:9-10 u:3-5 y:0-256:10-11 u:6-7 y:0-256:11-12 u:8-9 "
+             "y:0-256:12-13 u:10-11 y:0-256:13-16 t:0-64",
+    "main": "F at D0 xa:0-32 xv:32-64 xa:64-96 xv:96-128 xa:128-192 xv:192-224 xa:224-256 S:0-64 S:64-128 S:128-192 S:192-256 "
+            "ma:128-168 o sa:0-32 c:168-256 c:0-64 c:64-128 c:128-168 p O B sa:32-64 sa:64-128 sa:128-192 sa:192-256 "
+            "y:0-256:0-1 h y:0-256:1-2 U y:0-256:2-8 u:0-1 y:0-256:8-9 u:1-3 y:0-256:9-10 u:3-5 y:0-256:10-11 u:6-7 "
+            "y:0-256:11-12 u:8-9 y:0-256:12-13 u:10-11 y:0-256:13-16 t:0-64",
+    "tail": "fv new t:64-128 V tm l1 t:128-192 Z:0-192 t:192-256 Z:192-256 u:12-13 u:5-6 u:7-8 u:9-10 u:11-12",
+    "window": "ob ma:0-64 n mv:168-256 ma:64-128",
+    "m_early": 0,
+}
+
+
+def rank_program(g, core, T, topo):
+    rank = T.rank_of(core)
+    if rank is None:
+        return
+    N = len(T.cores)
+    Q = {"v": g.vector, "a": g.scalar, "t": g.tensor, "g": g, "s": g.sync}
+    CNT = {"v": "cv", "a": "ca", "t": "ct", "g": "cg"}
+    ops = []
+    recs = {}
+    seen = {q: {} for q in Q}
+    totals = {}
+
+    def A(name, lo=0, hi=None, step=1):
+        hi = SCRATCH[name][1][1] if hi is None else hi
+        ap = T[name][:, lo:hi] if step == 1 else T[name][:, lo:hi:step]
+        return (ap, name, lo, hi, step)
+
+    def IND(win, off):
+        return (win[0].indirect(off[0]), win[1], win[2], win[3], 2, off)
+
+    def note(a, writes, token, q):
+        rl = recs.setdefault(a[1], [])
+        if writes and a[4] == 1 and SCRATCH[a[1]][0] != "psum":
+            rl[:] = [r for r in rl if not (a[2] <= r[0] and r[1] <= a[3])]
+        rl.append((a[2], a[3], writes, token, q))
+
+    def emit(q, call, reads, writes, own=None):
+        reads = list(reads) + [a[5] for a in list(reads) + list(writes) if len(a) > 5]
+        need = {}
+        for a, wr in [(a, False) for a in reads] + [(a, True) for a in writes]:
+            psum = SCRATCH[a[1]][0] == "psum"
+            for lo, hi, w, tok, rq in recs.get(a[1], []):
+                if psum and rq != q:
+                    hit = True
+                elif psum and q == "t":
+                    hit = False
+                else:
+                    hit = (w or wr) and lo < a[3] and a[2] < hi
+                if hit and tok[1] > need.get(tok[0], -1):
+                    need[tok[0]] = tok[1]
+        waits = []
+        for s, v in need.items():
+            if seen[q].get(s, -1) < v:
+                seen[q][s] = v
+                waits.append((s, v))
+                if s in CNT:
+                    ops[v][3] = True
+        token = (q, len(ops)) if own is None else own
+        ops.append([q, call, waits, False, own])
+        for a in reads:
+            note(a, False, token, q if own is None else "dma")
+        for a in writes:
+            note(a, True, token, q if own is None else "dma")
+
+    def col(s):
+        return [s] if isinstance(s, tuple) else []
+
+    def val(s):
+        return s[0] if isinstance(s, tuple) else s
+
+    def cp(out, a):
+        emit("v", lambda: g.vector.tensor_copy(out[0], a[0]), [a], [out])
+
+    def tt(out, a, b, op):
+        emit("v", lambda: g.vector.tensor_tensor(out[0], a[0], b[0], op), [a, b], [out])
+
+    def ts(out, a, s1, op0, s2=None, op1=None):
+        if op1 is None:
+            emit("v", lambda: g.vector.tensor_scalar(out[0], a[0], val(s1), None, op0), [a] + col(s1), [out])
+        else:
+            emit("v", lambda: g.vector.tensor_scalar(out[0], a[0], val(s1), val(s2), op0, op1), [a] + col(s1) + col(s2), [out])
+
+    def fill(out, c):
+        emit("v", lambda: g.vector.memset(out[0], c), [], [out])
+
+    def act(out, a, bias=None, scale=1.0, fn=Fn.Identity, acc=None):
+        if bias is None:
+            emit("a", lambda: g.scalar.activation(out[0], a[0], Fn.Copy), [a], [out])
+        elif acc is None:
+            emit("a", lambda: g.scalar.activation(out[0], a[0], fn, bias=val(bias), scale=val(scale)),
+                 [a] + col(bias) + col(scale), [out])
+        else:
+            emit("a", lambda: g.scalar.activation(out[0], a[0], fn, bias=val(bias), scale=scale, accum_out=acc[0]),
+                 [a] + col(bias), [out, acc])
+
+    def mm(out, lhs, rhs, start, stop):
+        emit("t", lambda: g.tensor.matmul(out[0], lhs[0], rhs[0], start, stop), [lhs, rhs], [out])
+
+    def iota(out, pattern, mult, small=True):
+        if small:
+            emit("g", lambda: g.iota(out[0], pattern, 0, mult, allow_small_or_imprecise_dtypes=True), [], [out])
+        else:
+            emit("g", lambda: g.iota(out[0], pattern, 0, mult), [], [out])
+
+    def load(q, out, src, sem):
+        totals[sem] = 16
+        emit(q, lambda: Q[q].dma_start(out[0], src).then_inc(T.sem[sem], 16), [], [out], own=(sem, 16))
+
+    def store(q, dst, a, sem):
+        totals[sem] = 16
+        emit(q, lambda: Q[q].dma_start(dst, a[0]).then_inc(T.sem[sem], 16), [a], [], own=(sem, 16))
+
+    def send(a, to, land, rsem, lsem, after=()):
+        dst = T.cores[to]
+        rid, pid, se = topo.addr(dst)
+        totals[lsem] = totals.get(lsem, 0) + len(topo.engines(core, dst))
+        emit("g", lambda: g.remote_dma(land[0], a[0], T.sem[rsem], T.sem[lsem], pid, rid, topo.mask(core, dst)),
+             [a] + list(after), [], own=(lsem, totals[lsem]))
+
+    def expect(land, frm, rsem):
+        totals[rsem] = len(topo.engines(T.cores[frm], core))
+        note(land, True, (rsem, totals[rsem]), "dma")
+
+    def dest(t):
+        return (rank + 1 + t % (N - 1)) % N
+
+    def source(t):
+        return (rank - 1 - t % (N - 1)) % N
+
+    for t in range(RO):
+        expect(A("MR", t * VX, t * VX + V), dest(t), "am%d" % t)
+        expect(A("FR", t * L, (t + 1) * L), dest(t), "an%d" % t)
+        expect(A("L1R", t * 16, (t + 1) * 16), source(t), "a1%d" % t)
+        expect(A("CHR", t * L, (t + 1) * L), source(t), "a2%d" % t)
+
+    load("s", A("M", 0, V), T.mk[:], "d_mk")
+    load("s", A("SU", 0, V // 2), T.su[:, 0:V // 2], "d_su")
+    load("s", A("SU", V // 2, V), T.su[:, V // 2:V], "d_su2")
+    load("s", A("PL"), T.pl[:], "d_pl")
+    load("s", A("X", 0, W), T.xf[:], "d_x")
+    load("s", A("ST", 0, W), T.stp[:], "d_s")
+    load("a", A("HP"), T.hp[:], "d_hp")
+    load("a", A("TH", 0, RO), T.th[:], "d_th")
+    load("a", A("CP", 0, 1), T.cp[:], "d_cp")
+    load("s", A("X", W, WX), T.xf[:, 0:WX - W], "d_xe")
+    load("s", A("ST", W, WX), T.stp[:, 0:WX - W], "d_se")
+
+    def send_levels(t):
+        after = [A("CHR", (t - 1) * L, t * L)] if t else []
+        send(A("M", 0, V), source(t), A("MR", t * VX, t * VX + V), "am%d" % t, "lm", after)
+
+    iota(A("ip", 0, 1), [[0, 1]], 1, False)
+    iota(A("ion"), [[1, 144]], 0)
+    iota(A("iog"), [[1, 8], [0, 16]], 0)
+    iota(A("io16"), [[1, 16]], 0)
+    iota(A("seg"), [[0, 96], [15, 16]], 0)
+    send_levels(0)
+    ip = A("ip", 0, 1)
+
+    def KI(k):
+        return A("KI", k, k + 1)
+
+    def KF(k):
+        return A("KF", k, k + 1)
+
+    def KD(k):
+        return A("KD", k, k + 1)
+
+    def MAT(k):
+        return A("MAT", 128 * k, 128 * (k + 1))
+
+    fill(A("M", V, VX), 0.0)
+    for t in range(RO):
+        act(A("MR", t * VX + V, (t + 1) * VX), A("M", V, VX))
+    act(A("P", V, VX), A("M", V, VX))
+    ts(KI(0), ip, 127, Op.bitwise_and)
+    ts(KI(1), ip, 15, Op.bitwise_and)
+    ts(KI(2), ip, 112, Op.bitwise_and)
+    ts(KI(3), ip, 16, Op.bitwise_and)
+    ts(KI(4), ip, 1, Op.bitwise_and)
+    ts(KI(5), ip, 1, Op.arith_shift_right, 7, Op.bitwise_and)
+    ts(KI(6), ip, 4, Op.arith_shift_right)
+    cp(A("KF", 0, 7), A("KI", 0, 7))
+    kp, kr, kg, kh, kc, kr2, kgi = [KF(k) for k in range(7)]
+    gE, hs, gS, psw, wt, m0, m1, n0, n1, xr, r24, cb, jb0, jb1 = [KD(k) for k in range(14)]
+    ts(gE, kg, 15.0, Op.add)
+    ts(hs, kh, -2.0, Op.mult, 16.0, Op.add)
+    ts(wt, kr, 2.0, Op.mult, 1.0, Op.add)
+    ts(m1, kh, 1.0 / 16, Op.mult)
+    ts(r24, kr2, 4.0, Op.mult)
+    ts(gS, hs, gE, Op.add)
+    ts(psw, hs, kp, Op.add)
+    ts(xr, m1, kc, Op.not_equal)
+    i128 = A("ion", 0, 128)
+    ts(MAT(0), i128, kp, Op.is_equal)
+    ts(cb, xr, 512.0, Op.mult, r24, Op.add)
+    ts(MAT(1), i128, psw, Op.is_equal)
+    ts(A("WE"), A("ion"), gE, Op.is_equal)
+    ts(A("WS"), A("ion"), gS, Op.is_equal, wt, Op.mult)
+    ts(MAT(10), A("iog"), kgi, Op.is_equal)
+    ts(A("pq", 0, 16), A("io16"), 32.0, Op.mult, cb, Op.add)
+    ts(A("pq", 16, 32), A("io16"), 16.0, Op.mult, kr, Op.add)
+    for q in range(4):
+        ts(A("O2", 16 * q, 16 * q + 16), A("pq", 0, 16), float(q), Op.add)
+    ts(A("dl"), A("pq", 16, 32), -1.0 / 2048, Op.mult)
+
+    def scaled_constants():
+        act(A("WH"), A("WE"), 0.0, 0.5)
+        act(A("IF"), MAT(0))
+        act(A("WW"), A("WE"), 0.0, wt)
+        act(MAT(11), MAT(0), 0.0, 0.0)
+
+    def step_constants():
+        act(m0, kh, 1.0, -1.0 / 16)
+        act(n1, kh, 0.0, -1.0 / 16)
+        act(n0, kh, -1.0, 1.0 / 16)
+        act(jb0, kr, kh, 32.0)
+        act(jb1, jb0, hs)
+        for k, (m, mk) in enumerate([(0, m0), (0, m1), (1, m1), (1, m0), (0, n0), (0, n1), (1, n1), (1, n0)]):
+            act(MAT(2 + k), MAT(m), 0.0, mk)
+        act(A("jb", 0, 8), A("io16", 0, 8), jb1, 512.0)
+        act(A("jb", 8, 16), A("io16", 0, 8), jb0, 512.0)
+
+    def PU(lo, hi):
+        return A("pU", lo, hi)
+
+    def input_constants():
+        ts(A("hc"), A("HP"), -1.0 / 2048, Op.mult, 0.5, Op.add)
+        cp(A("thf", 0, RO), A("TH", 0, RO))
+        cp(A("capa", 0, 1), A("CP", 0, 1))
+        tt(A("hd", 0, 16), A("hc", 16, 32), A("hc", 0, 16), Op.subtract)
+        tt(A("rr"), A("hc", 48, 64), A("hc", 32, 48), Op.subtract)
+        tt(A("he", 16, 32), A("hc", 32, 48), A("hc", 0, 16), Op.subtract)
+        tt(A("hd", 16, 32), A("rr"), A("hd", 0, 16), Op.subtract)
+
+    def scaled_inputs():
+        act(A("he", 0, 16), A("hc", 0, 16), 8.0)
+        act(A("th2", 16, 16 + RO), A("thf", 0, RO), 0.5, -1.0)
+        act(A("cpf", 0, 1), A("capa", 0, 1), 1088.0)
+
+    def su_list(q, lo, hi):
+        cp(A("SL", q * L + lo, q * L + hi), A("SU", 4 * lo + q, 4 * hi, 4))
+
+    def gm_piece(e, t, lo, hi):
+        q = t % 4
+        src = IND(A("M", 0, V), A("SL", q * L + lo, q * L + hi))
+        if e == "a":
+            act(A("gm", 16 * lo, 16 * hi), src, -4.0)
+        else:
+            ts(A("gm", 16 * lo, 16 * hi), src, -4.0, Op.add)
+
+    def scan(lo, hi):
+        o, d0, d1 = A("sc", 16 * lo, 16 * hi), A("seg", 0, 16 * (hi - lo)), A("gm", 16 * lo, 16 * hi)
+        emit("v", lambda: g.vector.tensor_tensor_scan(o[0], d0[0], d1[0], 0.0, Op.min, Op.max), [d0, d1], [o])
+
+    def E(name, r):
+        return A(name, 15 - r, 143 - r)
+
+    def old_levels(t):
+        act(A("nold"), A("M", t % 4, V, 4), 7.5, -1.0, Fn.Sign)
+        mm(A("pC", 0, 16), MAT(0), A("dl"), True, False)
+        for r in range(16):
+            mm(A("pC", 0, 16), E("WH", r), A("nold", r, L, 16), False, False)
+
+    for t in range(RO):
+        q = t % 4
+        last = t == RO - 1
+        wx = W if t == 0 else WX
+        lanesM, lanesP = A("M", q, V, 4), A("P", q, V, 4)
+        th = A("thf", t, t + 1)
+        new = A("NEW", t * L, (t + 1) * L)
+        l1 = A("L1", t * 16, (t + 1) * 16)
+
+        def turn(lo, hi):
+            o, i = A("skT", 16 * lo, 16 * hi), A("sk", 16 * lo, 16 * hi)
+            emit("v", lambda: g.vector.transpose(o[0], i[0]), [i], [o])
+
+        small = [
+            lambda: cp(A("ui", 8, 24), PU(8, 24)),
+            lambda: ts(A("b0", 0, 16), A("ui", 8, 24), 4, Op.arith_shift_right, 1, Op.bitwise_and),
+            lambda: ts(A("b0", 16, 32), A("ui", 8, 24), 4, Op.arith_shift_right, 1, Op.bitwise_and),
+            lambda: ts(A("b1"), A("ui", 8, 24), 5, Op.arith_shift_right, 1, Op.bitwise_and),
+            lambda: tt(A("pq"), A("b0"), A("hd"), Op.mult),
+            lambda: ts(A("jj"), A("ui", 0, 16), 15, Op.bitwise_and),
+            lambda: tt(A("pr"), A("pq"), A("he"), Op.add),
+            lambda: ts(A("jm"), A("jj"), 1.0, Op.max),
+            lambda: tt(A("rr"), A("b1"), A("pr", 16, 32), Op.mult),
+            lambda: tt(A("ja"), A("jm"), A("jb"), Op.add),
+            lambda: tt(A("cc"), A("rr"), A("pr", 0, 16), Op.add),
+            lambda: cp(A("jl"), A("ja")),
+            lambda: cp(A("ui", 0, 8), PU(0, 8)),
+            lambda: cp(A("ui"), PU(0, 24)),
+        ]
+        def sums(lo, hi):
+            return A("pS" if lo < PLAN["split"] else "pA", lo, hi)
+
+        done = [0]
+
+        def burden(a, lo, hi):
+            mm(A("pL", lo, hi), E("WE", a), A("y", a * L + lo, a * L + hi), done[0] % 16 == 0, done[0] % 16 == 15)
+            done[0] += 1
+
+        def items(script, tm=t):
+            for word in script.split():
+                part = word.split(":")
+                n = part[0]
+                lo, hi = [int(v) for v in part[1].split("-")] if len(part) > 1 else (0, L)
+                if n == "xa":
+                    act(A("xk", 16 * lo, 16 * hi), IND(A("X", 0, wx), A("offs", lo, hi)))
+                elif n == "xv":
+                    cp(A("xk", 16 * lo, 16 * hi), IND(A("X", 0, wx), A("offs", lo, hi)))
+                elif n == "sa":
+                    act(A("sk", 16 * lo, 16 * hi), IND(A("ST", 0, wx), A("offs2", lo, hi)))
+                elif n == "sv":
+                    cp(A("sk", 16 * lo, 16 * hi), IND(A("ST", 0, wx), A("offs2", lo, hi)))
+                elif n in ("ma", "mv"):
+                    gm_piece(n[1], tm, lo, hi)
+                elif n == "c":
+                    scan(lo, hi)
+                elif n == "S":
+                    for a in range(16):
+                        mm(sums(lo, hi), MAT(0), A("xk", 16 * lo + a, 16 * hi, 16), a == 0, a == 15)
+                elif n == "O":
+                    ts(A("pO", lo, hi), sums(lo, hi), A("capa", 0, 1), Op.is_gt)
+                elif n == "B":
+                    act(A("Sb", lo, hi), sums(lo, hi))
+                elif n == "y":
+                    a0, a1 = [int(v) for v in part[2].split("-")]
+                    for a in range(a0, a1):
+                        ya = A("y", a * L + lo, a * L + hi)
+                        tt(ya, A("xk", 16 * lo + a, 16 * hi, 16), A("pO", lo, hi), Op.mult)
+                        burden(a, lo, hi)
+                elif n == "D0":
+                    mm(A("pD", 0, L), MAT(11), A("seg", 0, L), True, False)
+                elif n == "U":
+                    for r in range(16):
+                        mm(PU(8, 24), E("WW", r), A("Sb", r, L, 16), r == 0, r == 15)
+                elif n == "V":
+                    for r in range(16):
+                        mm(PU(0, 8), E("WS", r), A("Sb", 128 + r, L, 16), r == 0, r == 15)
+                elif n == "p":
+                    tt(A("pre"), A("sc", 15, 4096, 16), lanesM, Op.max)
+                elif n == "h":
+                    ts(A("thp"), A("pre"), 8.0, Op.is_lt, th, Op.mult)
+                elif n == "t":
+                    turn(lo, hi)
+                elif n == "u":
+                    for step in small[lo:hi]:
+                        step()
+                elif n == "o":
+                    cp(A("offs2"), IND(A("P" if t else "PL", 0, V), A("O2", 16 * q, 16 * q + 16)))
+                elif n == "Z":
+                    for bank, m in (("pD", 6), ("pZ", 2)):
+                        for x in range(2):
+                            for h in range(2):
+                                mm(A(bank, 128 * x + lo // 2, 128 * x + hi // 2), MAT(m + 2 * x + h),
+                                   A("skT", 16 * lo + 16 * h, 16 * hi, 32), False, False)
+                elif n == "fv":
+                    ts(A("f15"), A("pL", 0, L), th, Op.is_ge, 15.0, Op.mult)
+                elif n == "fa":
+                    act(A("sg"), A("pL", 0, L), A("th2", 16 + t, 17 + t), 1.0, Fn.Sign)
+                    act(A("f15"), A("sg"), 7.5, 7.5)
+                elif n == "new":
+                    tt(new, A("f15"), A("pre"), Op.max)
+                    send(new, source(t), A("FR", t * L, (t + 1) * L), "an%d" % t, "ln")
+                    act(lanesM, new)
+                elif n == "tm":
+                    tt(A("tm"), A("pC", 0, 16), A("cc"), Op.min)
+                elif n == "l1":
+                    ts(l1, A("tm"), -2048.0, Op.mult, float(V + 8 * 2048), Op.add)
+                    send(l1, dest(t), A("L1R", t * 16, (t + 1) * 16), "a1%d" % t, "l1")
+                elif n == "ob" and not last:
+                    act(A("ob"), A("tm"), -8.0 - 1.0 / 4096, 1.0, Fn.Sign)
+                    mm(A("pA", 0, 16), MAT(10), A("ob"), True, True)
+                    items("A")
+                elif n == "n":
+                    old_levels(tm)
+                elif n == "A":
+                    act(A("aw"), A("pA", 0, 16), 8.0, 0.5, Fn.Identity, A("af", 0, 1))
+                    act(A("ak", 0, 1), A("af", 0, 1), 135.5625, 0.125)
+                    act(A("af", 2, 3), A("af", 0, 1), A("cpf", 0, 1))
+                    act(A("capa", 0, 1), A("ak", 0, 1), A("af", 2, 3), -8.0)
+                elif n == "F":
+                    cp(A("offs"), lanesP if t else A("PL", 0, V, 4))
+                elif n == "at":
+                    mm(A("pZ", 0, L), A("IF"), lanesP, True, False)
+                elif n == "PC":
+                    cp(A("P", 0, V), A("PL"))
+                elif n == "L":
+                    su_list(tm % 4, lo, hi)
+                elif n == "SC":
+                    scaled_constants()
+                elif n == "SD":
+                    step_constants()
+                elif n == "IC":
+                    input_constants()
+                elif n == "SI":
+                    scaled_inputs()
+
+        items(PLAN["main0" if t == 0 else "main"])
+
+        tt(A("hi"), A("pL", 0, L), A("thp"), Op.is_ge)
+        for r in range(16):
+            mm(A("pC", 0, 16), E("WE", r), A("hi", r, L, 16), False, r == 15)
+        items(PLAN["tail"])
+
+        act(A("R"), IND(A("skT"), A("jl")))
+        for x in range(2):
+            mm(A("pD", 128 * x, 128 * x + 128), MAT(x), A("R", 128 - 128 * x, 256 - 128 * x), False, x == 1)
+        l1r = A("L1R", t * 16, (t + 1) * 16)
+
+        def clear():
+            cp(IND(A("M"), l1r), A("MR", V, VX))
+
+        def merge():
+            tt(lanesM, lanesM, A("back"), Op.max)
+
+        if t < 3:
+            su_list(t + 1, 0, L)
+        act(A("MR", t * VX + q, t * VX + V, 4), A("FR", t * L, (t + 1) * L))
+        act(A("back"), IND(A("MR", t * VX, (t + 1) * VX), l1), -4.0)
+        early = PLAN["m_early"]
+        if early >= 1:
+            clear()
+        tt(A("tt1"), A("pD", 0, L), A("hi"), Op.mult)
+        mm(A("pZ", 0, L), MAT(0), A("tt1"), False, True)
+        if early >= 2:
+            merge()
+        ch = A("CH", t * L, (t + 1) * L)
+        if last:
+            ts(A("t2"), A("pZ", 0, L), float(W), Op.is_ge, -float(W), Op.mult)
+            tt(A("t3"), A("pZ", 0, L), A("t2"), Op.add)
+            cp(ch, A("t3"))
+        else:
+            cp(ch, A("pZ", 0, L))
+        send(ch, dest(t), A("CHR", t * L, (t + 1) * L), "a2%d" % t, "l2")
+        if early < 1:
+            clear()
+        if early < 2:
+            merge()
+        if not last:
+            send_levels(t + 1)
+            items(PLAN["window"], t + 1)
+            cp(IND(A("P"), l1r), A("CHR", t * L, (t + 1) * L))
+        else:
+            store("s", T.ymk[:], A("M", 0, V), "d_om")
+            for k, bank in enumerate(("pS", "pO")):
+                ts(A(bank), A("P", 512 * k, 512 * k + 512), float(W), Op.is_ge, -float(W), Op.mult)
+            for k, bank in enumerate(("pS", "pO")):
+                tt(A("P", 512 * k, 512 * k + 512), A(bank), A("P", 512 * k, 512 * k + 512), Op.add)
+            cp(IND(A("P"), l1r), A("CHR", t * L, (t + 1) * L))
+            store("s", T.ypl[:], A("P", 0, V), "d_op")
+
+    number = {}
+    count = {q: 0 for q in CNT}
+    for k, (q, call, waits, marked, own) in enumerate(ops):
+        if marked:
+            count[q] += 1
+            number[k] = count[q]
+    for k, (q, call, waits, marked, own) in enumerate(ops):
+        for s, v in waits:
+            if s in CNT:
+                Q[q].wait_ge(T.sem[CNT[s]], number[v])
+            else:
+                Q[q].wait_ge(T.sem[s], v)
+        ins = call()
+        if marked:
+            ins.then_inc(T.sem[CNT[q]], 1)
+    for s, v in totals.items():
+        g.wait_ge(T.sem[s], v)

@@ -15,17 +15,18 @@ SCRATCH = {
     "SU": _sb(V, I32), "SL": _sb(V, U16), "HP": _sb(64, I32), "CP": _sb(4, I32), "TH": _sb(8, I32),
     "hc": _sb(64, F32), "hd": _sb(32, F32), "he": _sb(32, F32), "cpf": _sb(4, F32), "thf": _sb(8, F32), "capa": _sb(4, F32),
     "xk": _sb(4096, BF), "sk": _sb(4096, BF), "skT": _sb(4096, BF), "gm": _sb(4096, BF), "sc": _sb(4096, BF), "y": _sb(4096, BF),
-    "seg": _sb(1536, BF), "offs": _sb(L, U16), "offs2": _sb(L, U16), "O2": _sb(64, U16),
+    "seg": _sb(1536, BF), "offs": _sb(L, U16), "Sm": _sb(L, BF),
     "Sb": _sb(L, BF), "pre": _sb(L, BF), "thp": _sb(L, BF), "nold": _sb(L, BF), "hi": _sb(L, BF), "f15": _sb(L, BF),
     "R": _sb(L, BF), "tt1": _sb(L, BF), "t2": _sb(L, F32), "t3": _sb(L, F32), "back": _sb(L, BF),
-    "ui": _sb(24, I32), "b0": _sb(32, I32), "b1": _sb(16, I32), "pq": _sb(32, F32), "pr": _sb(32, F32), "rr": _sb(16, F32),
+    "ui": _sb(32, I32), "b0": _sb(32, I32), "b1": _sb(16, I32), "pq": _sb(32, F32), "pr": _sb(32, F32), "rr": _sb(16, F32),
     "cc": _sb(16, F32), "jj": _sb(16, I32), "jm": _sb(16, F32), "ja": _sb(16, F32), "jl": _sb(16, U16), "jb": _sb(16, F32),
     "tm": _sb(16, F32), "ob": _sb(16, BF), "af": _sb(4, F32), "aw": _sb(16, F32), "ak": _sb(8, BF), "dl": _sb(16, BF),
     "NEW": _sb(RO * L, BF), "L1": _sb(RO * 16, U16), "CH": _sb(RO * L, U16),
     "MR": _sb(RO * VX, BF), "FR": _sb(RO * L, BF), "L1R": _sb(RO * 16, U16), "CHR": _sb(RO * L, U16),
     "ip": _sb(4, I32), "KI": _sb(8, I32), "KF": _sb(8, F32), "KD": _sb(16, F32),
     "ion": _sb(144, BF), "iog": _sb(128, BF), "io16": _sb(16, F32),
-    "WE": _sb(144, BF), "WW": _sb(144, BF), "WS": _sb(144, BF), "WH": _sb(144, BF), "MAT": _sb(12 * 128, BF),
+    "WE": _sb(144, BF), "WW": _sb(144, BF), "WS": _sb(144, BF), "WH": _sb(144, BF), "MAT": _sb(14 * 128, BF), "ov": _sb(L, BF),
+    "yh": _sb(2048, "float16"), "WZ": _sb(144, "float16"), "WL": _sb(144, "float16"), "kk": _sb(L, BF), "CT": _sb(L, BF),
     "sg": _sb(L, BF), "th2": _sb(24, F32),
     "pS": ("psum", [128, 512], F32), "pO": ("psum", [128, 512], F32), "pL": ("psum", [128, 512], F32),
     "pU": ("psum", [128, 512], F32), "pC": ("psum", [128, 512], F32), "pZ": ("psum", [128, 512], F32),
@@ -36,18 +37,19 @@ SEMAPHORES = (["cv", "ca", "ct", "cg"] + LOADS + ["lm", "ln", "l1", "l2"]
               + ["%s%d" % (k, t) for k in ("am", "an", "a1", "a2") for t in range(RO)])
 
 PLAN = {
-    "split": 256,
-    "main0": "SC L:0-128 ma:0-64 mv:64-128 L:128-256 ma:128-192 IC F ma:192-256 c:0-64 c:64-128 c:128-192 n SI D0 "
-             "xa:0-32 xv:32-64 xa:64-96 xv:96-128 xa:128-192 xv:192-256 S:0-64 S:64-128 S:128-192 S:192-256 "
-             "o c:192-256 PC at p h O B sa:0-64 sa:64-128 sa:128-192 sa:192-256 SD "
-             "y:0-256:0-2 U y:0-256:2-8 u:0-1 y:0-256:8-9 u:1-3 y:0-256:9-10 u:3-5 y:0-256:10-11 u:6-7 y:0-256:11-12 u:8-9 "
-             "y:0-256:12-13 u:10-11 y:0-256:13-16 t:0-64",
-    "main": "F at D0 xa:0-32 xv:32-64 xa:64-96 xv:96-128 xa:128-192 xv:192-224 xa:224-256 S:0-64 S:64-128 S:128-192 S:192-256 "
-            "ma:128-168 o sa:0-32 c:168-256 c:0-64 c:64-128 c:128-168 p O B sa:32-64 sa:64-128 sa:128-192 sa:192-256 "
-            "y:0-256:0-1 h y:0-256:1-2 U y:0-256:2-8 u:0-1 y:0-256:8-9 u:1-3 y:0-256:9-10 u:3-5 y:0-256:10-11 u:6-7 "
-            "y:0-256:11-12 u:8-9 y:0-256:12-13 u:10-11 y:0-256:13-16 t:0-64",
-    "tail": "fv new t:64-128 V tm l1 t:128-192 Z:0-192 t:192-256 Z:192-256 u:12-13 u:5-6 u:7-8 u:9-10 u:11-12",
-    "window": "ob ma:0-64 n mv:168-256 ma:64-128",
+    "split": 256, "pack": 0,
+    "main0": "SC L:0-128 ma:0-64 mv:64-128 L:128-256 ma:128-192 IC F ma:192-256 c:0-64 c:64-128 PC c:128-192 n SI D0 "
+             "xa:0-32 xv:32-64 xa:64-96 xv:96-128 xa:128-160 xv:160-192 xa:192-224 xv:224-256 "
+             "S:0-64 S:64-128 S:128-192 S:192-256 c:192-256 p sa:0-32 O B U sa:32-96 Vm Ve sa:96-192 sa:192-256 SD "
+             "y:0-4 u:0-1 y:4-5 V at u:1-2 y:5-6 u:2-3 y:6-7 u:3-4 h y:7-8 u:4-5 y:8-9 u:12-13 y:9-10 u:6-7 y:10-11 u:5-6 "
+             "y:11-12 u:8-9 y:12-13 u:7-8 y:13-14 u:10-11 y:14-15 u:9-10 y:15-16 u:11-12 t:0-24",
+    "main": "F D0 at xa:0-32 xv:32-64 xa:64-96 xv:96-128 xv:128-160 xa:160-192 xa:192-224 xv:224-256 "
+            "S:0-64 S:64-128 S:128-192 S:192-256 ma:112-152 c:200-256 c:0-56 c:56-112 O B U Vm ma:152-200 Ve "
+            "sa:0-64 sa:64-128 sa:128-192 sa:192-256 y:0-4 u:0-1 y:4-5 V u:1-2 c:112-200 y:5-6 u:2-3 p y:6-7 u:3-4 h "
+            "y:7-8 u:4-5 y:8-9 u:12-13 y:9-10 u:6-7 y:10-11 u:5-6 y:11-12 u:8-9 y:12-13 u:7-8 y:13-14 u:10-11 "
+            "y:14-15 u:9-10 y:15-16 u:11-12 t:0-24",
+    "tail": "fv new t:24-64 tm l1 t:64-128 Z:0-128 t:128-192 Z:128-192 R:0-192 t:192-256 Z:192-256 R:192-256",
+    "window": "ob mv:200-256 ma:0-56 n ma:56-112",
     "m_early": 0,
 }
 
@@ -221,52 +223,57 @@ def rank_program(g, core, T, topo):
     ts(KI(1), ip, 15, Op.bitwise_and)
     ts(KI(2), ip, 112, Op.bitwise_and)
     ts(KI(3), ip, 16, Op.bitwise_and)
-    ts(KI(4), ip, 1, Op.bitwise_and)
-    ts(KI(5), ip, 1, Op.arith_shift_right, 7, Op.bitwise_and)
-    ts(KI(6), ip, 4, Op.arith_shift_right)
-    cp(A("KF", 0, 7), A("KI", 0, 7))
-    kp, kr, kg, kh, kc, kr2, kgi = [KF(k) for k in range(7)]
-    gE, hs, gS, psw, wt, m0, m1, n0, n1, xr, r24, cb, jb0, jb1 = [KD(k) for k in range(14)]
+    ts(KI(4), ip, 4, Op.arith_shift_right)
+    cp(A("KF", 0, 5), A("KI", 0, 5))
+    kp, kr, kg, kh, kgi = [KF(k) for k in range(5)]
+    gE, hs, psw, wt, m0, m1, jb0, jb1 = [KD(k) for k in range(8)]
     ts(gE, kg, 15.0, Op.add)
     ts(hs, kh, -2.0, Op.mult, 16.0, Op.add)
     ts(wt, kr, 2.0, Op.mult, 1.0, Op.add)
     ts(m1, kh, 1.0 / 16, Op.mult)
-    ts(r24, kr2, 4.0, Op.mult)
-    ts(gS, hs, gE, Op.add)
+    ts(m0, kh, -1.0 / 16, Op.mult, 1.0, Op.add)
     ts(psw, hs, kp, Op.add)
-    ts(xr, m1, kc, Op.not_equal)
     i128 = A("ion", 0, 128)
     ts(MAT(0), i128, kp, Op.is_equal)
-    ts(cb, xr, 512.0, Op.mult, r24, Op.add)
     ts(MAT(1), i128, psw, Op.is_equal)
     ts(A("WE"), A("ion"), gE, Op.is_equal)
-    ts(A("WS"), A("ion"), gS, Op.is_equal, wt, Op.mult)
+    for k, (tg, mk) in enumerate([(kp, m0), (kp, m1), (psw, m1), (psw, m0)]):
+        ts(MAT(2 + k), i128, tg, Op.is_equal, mk, Op.mult)
     ts(MAT(10), A("iog"), kgi, Op.is_equal)
-    ts(A("pq", 0, 16), A("io16"), 32.0, Op.mult, cb, Op.add)
     ts(A("pq", 16, 32), A("io16"), 16.0, Op.mult, kr, Op.add)
-    for q in range(4):
-        ts(A("O2", 16 * q, 16 * q + 16), A("pq", 0, 16), float(q), Op.add)
     ts(A("dl"), A("pq", 16, 32), -1.0 / 2048, Op.mult)
 
     def scaled_constants():
         act(A("WH"), A("WE"), 0.0, 0.5)
         act(A("IF"), MAT(0))
         act(A("WW"), A("WE"), 0.0, wt)
+        act(jb0, kr, kh, 32.0)
         act(MAT(11), MAT(0), 0.0, 0.0)
+        act(jb1, jb0, hs)
+        act(A("jb", 8, 16), A("io16", 0, 8), jb0, 512.0)
+        act(A("jb", 0, 8), A("io16", 0, 8), jb1, 512.0)
 
     def step_constants():
-        act(m0, kh, 1.0, -1.0 / 16)
-        act(n1, kh, 0.0, -1.0 / 16)
-        act(n0, kh, -1.0, 1.0 / 16)
-        act(jb0, kr, kh, 32.0)
-        act(jb1, jb0, hs)
-        for k, (m, mk) in enumerate([(0, m0), (0, m1), (1, m1), (1, m0), (0, n0), (0, n1), (1, n1), (1, n0)]):
-            act(MAT(2 + k), MAT(m), 0.0, mk)
-        act(A("jb", 0, 8), A("io16", 0, 8), jb1, 512.0)
-        act(A("jb", 8, 16), A("io16", 0, 8), jb0, 512.0)
+        for k in range(4):
+            act(MAT(6 + k), MAT(2 + k), 0.0, -1.0)
+
+    def pack_constants():
+        fh, gZ, r8, r9, ct = [KD(k) for k in range(8, 13)]
+        ts(fh, kr, 8.0, Op.is_ge, 8.0, Op.mult)
+        ts(A("WL"), A("ion"), gE, Op.is_equal)
+        ts(gZ, fh, gE, Op.add)
+        ts(r8, fh, -1.0, Op.mult, kp, Op.add)
+        ts(ct, fh, -4386.0, Op.mult, 34816.0, Op.add)
+        ts(A("WZ"), A("ion"), gZ, Op.is_equal)
+        ts(r9, r8, 8.0, Op.add)
+        ts(A("kk", 128, 256), i128, r8, Op.is_equal, -128.0, Op.mult)
+        ts(A("kk", 0, 128), i128, r9, Op.is_equal)
+        act(A("CT"), A("M", V, VX), ct)
+        act(MAT(12), MAT(0), 0.0, 128.0)
+        tt(MAT(13), A("kk", 128, 256), A("kk", 0, 128), Op.add)
 
     def PU(lo, hi):
-        return A("pU", lo, hi)
+        return A("pZ", L + lo, L + hi) if PLAN["pack"] else A("pU", lo, hi)
 
     def input_constants():
         ts(A("hc"), A("HP"), -1.0 / 2048, Op.mult, 0.5, Op.add)
@@ -280,6 +287,8 @@ def rank_program(g, core, T, topo):
     def scaled_inputs():
         act(A("he", 0, 16), A("hc", 0, 16), 8.0)
         act(A("th2", 16, 16 + RO), A("thf", 0, RO), 0.5, -1.0)
+        act(A("th2", 0, RO), A("thf", 0, RO), 0.0, 0.5)
+        act(A("th2", 8, 8 + RO), A("thf", 0, RO), 0.0, -0.5)
         act(A("cpf", 0, 1), A("capa", 0, 1), 1088.0)
 
     def su_list(q, lo, hi):
@@ -320,10 +329,10 @@ def rank_program(g, core, T, topo):
             emit("v", lambda: g.vector.transpose(o[0], i[0]), [i], [o])
 
         small = [
-            lambda: cp(A("ui", 8, 24), PU(8, 24)),
-            lambda: ts(A("b0", 0, 16), A("ui", 8, 24), 4, Op.arith_shift_right, 1, Op.bitwise_and),
-            lambda: ts(A("b0", 16, 32), A("ui", 8, 24), 4, Op.arith_shift_right, 1, Op.bitwise_and),
-            lambda: ts(A("b1"), A("ui", 8, 24), 5, Op.arith_shift_right, 1, Op.bitwise_and),
+            lambda: cp(A("ui", 16, 32), PU(16, 32)),
+            lambda: ts(A("b0", 0, 16), A("ui", 16, 32), 4, Op.arith_shift_right, 1, Op.bitwise_and),
+            lambda: ts(A("b0", 16, 32), A("ui", 16, 32), 4, Op.arith_shift_right, 1, Op.bitwise_and),
+            lambda: ts(A("b1"), A("ui", 16, 32), 5, Op.arith_shift_right, 1, Op.bitwise_and),
             lambda: tt(A("pq"), A("b0"), A("hd"), Op.mult),
             lambda: ts(A("jj"), A("ui", 0, 16), 15, Op.bitwise_and),
             lambda: tt(A("pr"), A("pq"), A("he"), Op.add),
@@ -332,11 +341,13 @@ def rank_program(g, core, T, topo):
             lambda: tt(A("ja"), A("jm"), A("jb"), Op.add),
             lambda: tt(A("cc"), A("rr"), A("pr", 0, 16), Op.add),
             lambda: cp(A("jl"), A("ja")),
-            lambda: cp(A("ui", 0, 8), PU(0, 8)),
-            lambda: cp(A("ui"), PU(0, 24)),
+            lambda: cp(A("ui", 0, 16), PU(0, 16)),
         ]
         def sums(lo, hi):
             return A("pS" if lo < PLAN["split"] else "pA", lo, hi)
+
+        def pair(a, lo, hi):
+            return A(("pO", "pA", "pU", "pD")[a // 2], a % 2 * L + lo, a % 2 * L + hi)
 
         done = [0]
 
@@ -354,9 +365,9 @@ def rank_program(g, core, T, topo):
                 elif n == "xv":
                     cp(A("xk", 16 * lo, 16 * hi), IND(A("X", 0, wx), A("offs", lo, hi)))
                 elif n == "sa":
-                    act(A("sk", 16 * lo, 16 * hi), IND(A("ST", 0, wx), A("offs2", lo, hi)))
+                    act(A("sk", 16 * lo, 16 * hi), IND(A("ST", 0, wx), A("offs", lo, hi)))
                 elif n == "sv":
-                    cp(A("sk", 16 * lo, 16 * hi), IND(A("ST", 0, wx), A("offs2", lo, hi)))
+                    cp(A("sk", 16 * lo, 16 * hi), IND(A("ST", 0, wx), A("offs", lo, hi)))
                 elif n in ("ma", "mv"):
                     gm_piece(n[1], tm, lo, hi)
                 elif n == "c":
@@ -369,19 +380,62 @@ def rank_program(g, core, T, topo):
                 elif n == "B":
                     act(A("Sb", lo, hi), sums(lo, hi))
                 elif n == "y":
-                    a0, a1 = [int(v) for v in part[2].split("-")]
+                    a0, a1 = [int(v) for v in part[-1].split("-")]
+                    if len(part) == 2:
+                        lo, hi = 0, L
                     for a in range(a0, a1):
                         ya = A("y", a * L + lo, a * L + hi)
                         tt(ya, A("xk", 16 * lo + a, 16 * hi, 16), A("pO", lo, hi), Op.mult)
                         burden(a, lo, hi)
+                elif n == "K":
+                    for a in range(8):
+                        mm(pair(a, lo, hi), MAT(0), A("xk", 16 * lo + a, 16 * hi, 16), True, False)
+                        mm(pair(a, lo, hi), MAT(12), A("xk", 16 * lo + a + 8, 16 * hi, 16), False, True)
+                elif n == "Bv":
+                    cp(A("Sb"), A("pS", 0, L))
+                elif n == "Os":
+                    ts(A("ov"), A("Sb"), A("capa", 0, 1), Op.is_gt)
+                elif n == "C0":
+                    mm(A("pL", 0, L), MAT(0), A("CT"), True, False)
+                elif n == "w":
+                    for a in range(lo, hi):
+                        ya = A("yh", a * L, (a + 1) * L)
+                        tt(ya, pair(a, 0, L), A("ov"), Op.mult)
+                        mm(A("pS", L, 2 * L), E("WZ", a), ya, done[0] == 0, done[0] == 7)
+                        mm(A("pL", 0, L), E("WL", a), ya, False, False)
+                        done[0] += 1
+                elif n == "k":
+                    ts(A("kk"), A("pS", L, 2 * L), 1.0 / 128, Op.mult, 136.0 - 63.5 / 128, Op.add)
+                    mm(A("pL", 0, L), MAT(13), A("kk"), False, True)
+                elif n == "KC":
+                    pack_constants()
+                elif n == "R":
+                    got = [A("R", 128 - 128 * x + lo // 2, 128 - 128 * x + hi // 2) for x in range(2)]
+                    if hi - lo == L:
+                        act(A("R"), IND(A("skT"), A("jl")))
+                    else:
+                        for x in range(2):
+                            act(got[x], IND(A("skT", 0, 16 * hi), A("jl", 8 - 8 * x + lo // 32, 8 - 8 * x + hi // 32)))
+                    for x in range(2):
+                        for h in range(2):
+                            mm(A("pD", lo + (h ^ x), hi, 2), MAT(2 + 2 * x + h), got[x], False, hi == L and x + h == 2)
                 elif n == "D0":
                     mm(A("pD", 0, L), MAT(11), A("seg", 0, L), True, False)
                 elif n == "U":
                     for r in range(16):
-                        mm(PU(8, 24), E("WW", r), A("Sb", r, L, 16), r == 0, r == 15)
+                        mm(PU(16, 32), E("WW", r), A("Sb", r, L, 16), r == 0, r == 15)
                 elif n == "V":
                     for r in range(16):
-                        mm(PU(0, 8), E("WS", r), A("Sb", 128 + r, L, 16), r == 0, r == 15)
+                        mm(PU(0, 16), E("WW", r), A("Sm", r, L, 16), r == 0, r == 15)
+                elif n == "Vm":
+                    for x in range(2):
+                        for c in range(2):
+                            mm(A("pA", L + 128 - 128 * x, 2 * L - 128 * x), MAT(2 + 2 * x + c), A("Sb", c, L, 2), c == 0, c == 1)
+                elif n == "Ve":
+                    act(A("Sm"), A("pA", L, 2 * L))
+                elif n == "ha":
+                    act(A("sg"), A("pre"), -7.5, 1.0, Fn.Sign)
+                    act(A("thp"), A("sg"), A("th2", t, t + 1), A("th2", 8 + t, 9 + t))
                 elif n == "p":
                     tt(A("pre"), A("sc", 15, 4096, 16), lanesM, Op.max)
                 elif n == "h":
@@ -391,13 +445,11 @@ def rank_program(g, core, T, topo):
                 elif n == "u":
                     for step in small[lo:hi]:
                         step()
-                elif n == "o":
-                    cp(A("offs2"), IND(A("P" if t else "PL", 0, V), A("O2", 16 * q, 16 * q + 16)))
                 elif n == "Z":
                     for bank, m in (("pD", 6), ("pZ", 2)):
                         for x in range(2):
                             for h in range(2):
-                                mm(A(bank, 128 * x + lo // 2, 128 * x + hi // 2), MAT(m + 2 * x + h),
+                                mm(A(bank, lo + (h ^ x), hi, 2), MAT(m + 2 * x + h),
                                    A("skT", 16 * lo + 16 * h, 16 * hi, 32), False, False)
                 elif n == "fv":
                     ts(A("f15"), A("pL", 0, L), th, Op.is_ge, 15.0, Op.mult)
@@ -448,9 +500,6 @@ def rank_program(g, core, T, topo):
             mm(A("pC", 0, 16), E("WE", r), A("hi", r, L, 16), False, r == 15)
         items(PLAN["tail"])
 
-        act(A("R"), IND(A("skT"), A("jl")))
-        for x in range(2):
-            mm(A("pD", 128 * x, 128 * x + 128), MAT(x), A("R", 128 - 128 * x, 256 - 128 * x), False, x == 1)
         l1r = A("L1R", t * 16, (t + 1) * 16)
 
         def clear():
@@ -489,7 +538,8 @@ def rank_program(g, core, T, topo):
         else:
             store("s", T.ymk[:], A("M", 0, V), "d_om")
             for k, bank in enumerate(("pS", "pO")):
-                ts(A(bank), A("P", 512 * k, 512 * k + 512), float(W), Op.is_ge, -float(W), Op.mult)
+                act(A("gm", 512 * k, 512 * k + 512), A("P", 512 * k, 512 * k + 512), 0.5 - W, 1.0, Fn.Sign)
+                act(A(bank), A("gm", 512 * k, 512 * k + 512), -W / 2.0, -W / 2.0)
             for k, bank in enumerate(("pS", "pO")):
                 tt(A("P", 512 * k, 512 * k + 512), A(bank), A("P", 512 * k, 512 * k + 512), Op.add)
             cp(IND(A("P"), l1r), A("CHR", t * L, (t + 1) * L))

@@ -1,9 +1,14 @@
-from concourse.mybir import AluOpType as Op, ActivationFunctionType as Fn, AxisListType as Ax
+import math
+from concourse.mybir import AluOpType as Op, ActivationFunctionType as Fn
 
 W, V, L, RO = 3840, 1024, 256, 6
 WX = 5120
 VX = V + L
 BF, F32, I32, U16 = "bfloat16", "float32", "int32", "uint16"
+BITS, LOW = 14, -84
+ZERO, DOWN, HIGH = 2.0 ** LOW, 2.0 ** (-4 * BITS), 2.0 ** 25
+HALF_TOP = 2.0 ** ((15 * BITS + LOW) // 2)
+LN2 = math.log(2.0)
 
 
 def _sb(n, d):
@@ -11,47 +16,40 @@ def _sb(n, d):
 
 
 SCRATCH = {
-    "X": _sb(WX, BF), "ST": _sb(WX, BF), "P": _sb(VX, F32), "PL": _sb(V, I32), "IF": _sb(128, F32), "M": _sb(VX, BF),
+    "X": _sb(WX, BF), "ST": _sb(WX, BF), "P": _sb(VX, F32), "PL": _sb(V, I32), "M": _sb(VX, BF),
     "SU": _sb(V, I32), "SL": _sb(V, U16), "HP": _sb(64, I32), "CP": _sb(4, I32), "TH": _sb(8, I32),
-    "hc": _sb(64, F32), "hd": _sb(32, F32), "he": _sb(32, F32), "cpf": _sb(4, F32), "thf": _sb(8, F32), "capa": _sb(4, F32),
-    "xk": _sb(4096, BF), "sk": _sb(4096, BF), "skT": _sb(4096, BF), "gm": _sb(4096, BF), "sc": _sb(4096, BF), "y": _sb(4096, BF),
-    "seg": _sb(1536, BF), "offs": _sb(L, U16), "Sm": _sb(L, BF),
-    "Sb": _sb(L, BF), "pre": _sb(L, BF), "thp": _sb(L, BF), "nold": _sb(L, BF), "hi": _sb(L, BF), "f15": _sb(L, BF),
-    "R": _sb(L, BF), "tt1": _sb(L, BF), "t2": _sb(L, F32), "t3": _sb(L, F32), "back": _sb(L, BF),
-    "ui": _sb(32, I32), "b0": _sb(32, I32), "b1": _sb(16, I32), "pq": _sb(32, F32), "pr": _sb(32, F32), "rr": _sb(16, F32),
-    "cc": _sb(16, F32), "jj": _sb(16, I32), "jm": _sb(16, F32), "ja": _sb(16, F32), "jl": _sb(16, U16), "jb": _sb(16, F32),
-    "tm": _sb(16, F32), "ob": _sb(16, BF), "af": _sb(4, F32), "aw": _sb(16, F32), "ak": _sb(8, BF), "dl": _sb(16, BF),
-    "NEW": _sb(RO * L, BF), "L1": _sb(RO * 16, U16), "CH": _sb(RO * L, U16),
+    "hc": _sb(64, F32), "hd": _sb(64, F32), "ht": _sb(64, F32), "hs": _sb(64, F32),
+    "cpf": _sb(4, F32), "thf": _sb(8, F32), "rem": _sb(4, F32),
+    "xk": _sb(4096, BF), "sk": _sb(4096, BF), "skT": _sb(4096, BF), "gm": _sb(4096, BF), "y": _sb(4096, BF),
+    "offs": _sb(L, U16), "SS": _sb(3 * L, BF), "ov": _sb(L, BF), "hi": _sb(L, BF), "f15": _sb(L, BF),
+    "R": _sb(L, BF), "tt1": _sb(L, BF), "t2": _sb(L, F32), "t3": _sb(L, F32), "zero": _sb(L, BF), "low": _sb(L, BF),
+    "MK": _sb(V, BF), "MO": _sb(VX, BF), "bk": _sb(L, BF),
+    "dc": _sb(1536, BF), "dh": _sb(1536, BF), "dw": _sb(1536, BF), "dr": _sb(1536, BF),
+    "ui": _sb(32, I32), "uw": _sb(32, I32), "jm": _sb(16, F32), "ja": _sb(16, F32), "jl": _sb(16, U16), "jb": _sb(16, F32),
+    "li": _sb(16, F32), "tm": _sb(16, F32), "ob": _sb(16, BF), "af": _sb(4, F32), "ak": _sb(8, BF), "dl": _sb(32, BF),
+    "NEW": _sb((RO + 1) * L, BF), "L1": _sb(RO * 16, U16), "CH": _sb(RO * L, U16),
     "MR": _sb(RO * VX, BF), "FR": _sb(RO * L, BF), "L1R": _sb(RO * 16, U16), "CHR": _sb(RO * L, U16),
-    "ip": _sb(4, I32), "KI": _sb(8, I32), "KF": _sb(8, F32), "KD": _sb(16, F32),
-    "ion": _sb(144, BF), "iog": _sb(128, BF), "io16": _sb(16, F32),
-    "WE": _sb(144, BF), "WW": _sb(144, BF), "WS": _sb(144, BF), "WH": _sb(144, BF), "MAT": _sb(14 * 128, BF), "ov": _sb(L, BF),
-    "yh": _sb(2048, "float16"), "WZ": _sb(144, "float16"), "WL": _sb(144, "float16"), "kk": _sb(L, BF), "CT": _sb(L, BF),
-    "sg": _sb(L, BF), "th2": _sb(24, F32),
-    "pS": ("psum", [128, 512], F32), "pO": ("psum", [128, 512], F32), "pL": ("psum", [128, 512], F32),
-    "pU": ("psum", [128, 512], F32), "pC": ("psum", [128, 512], F32), "pZ": ("psum", [128, 512], F32),
-    "pD": ("psum", [128, 512], F32), "pA": ("psum", [128, 512], F32),
+    "ip": _sb(4, I32), "KI": _sb(8, I32), "KF": _sb(8, F32), "KD": _sb(8, F32),
+    "ion": _sb(144, BF), "iog": _sb(128, BF), "io16": _sb(16, F32), "IF": _sb(128, F32), "BH": _sb(128, F32),
+    "WE": _sb(144, BF), "WN": _sb(144, BF), "WW": _sb(144, BF), "MAT": _sb(13 * 128, BF),
 }
+for _bank in ("pS", "pA", "pL", "pC", "pG", "pU", "pZ", "pD"):
+    SCRATCH[_bank] = ("psum", [128, 512], F32)
 LOADS = ["d_mk", "d_su", "d_su2", "d_pl", "d_x", "d_s", "d_xe", "d_se", "d_hp", "d_cp", "d_th", "d_om", "d_op"]
 SEMAPHORES = (["cv", "ca", "ct", "cg"] + LOADS + ["lm", "ln", "l1", "l2"]
               + ["%s%d" % (k, t) for k in ("am", "an", "a1", "a2") for t in range(RO)])
 
 PLAN = {
-    "split": 256, "pack": 0,
-    "main0": "SC L:0-128 ma:0-64 mv:64-128 L:128-256 ma:128-192 IC F ma:192-256 c:0-64 c:64-128 PC c:128-192 n SI D0 "
-             "xa:0-32 xv:32-64 xa:64-96 xv:96-128 xa:128-160 xv:160-192 xa:192-224 xv:224-256 "
-             "S:0-64 S:64-128 S:128-192 S:192-256 c:192-256 p sa:0-32 O B U sa:32-96 Vm Ve sa:96-192 sa:192-256 SD "
-             "y:0-4 u:0-1 y:4-5 V at u:1-2 y:5-6 u:2-3 y:6-7 u:3-4 h y:7-8 u:4-5 y:8-9 u:12-13 y:9-10 u:6-7 y:10-11 u:5-6 "
-             "y:11-12 u:8-9 y:12-13 u:7-8 y:13-14 u:10-11 y:14-15 u:9-10 y:15-16 u:11-12 t:0-24",
-    "main": "F D0 at xa:0-32 xv:32-64 xa:64-96 xv:96-128 xv:128-160 xa:160-192 xa:192-224 xv:224-256 "
-            "S:0-64 S:64-128 S:128-192 S:192-256 ma:112-152 c:200-256 c:0-56 c:56-112 O B U Vm ma:152-200 Ve "
-            "sa:0-64 sa:64-128 sa:128-192 sa:192-256 y:0-4 u:0-1 y:4-5 V u:1-2 c:112-200 y:5-6 u:2-3 p y:6-7 u:3-4 h "
-            "y:7-8 u:4-5 y:8-9 u:12-13 y:9-10 u:6-7 y:10-11 u:5-6 y:11-12 u:8-9 y:12-13 u:7-8 y:13-14 u:10-11 "
-            "y:14-15 u:9-10 y:15-16 u:11-12 t:0-24",
-    "tail": "fv new t:24-64 tm l1 t:64-128 Z:0-128 t:128-192 Z:128-192 R:0-192 t:192-256 Z:192-256 R:192-256",
-    "window": "ob mv:200-256 ma:0-56 n ma:56-112",
-    "m_early": 0,
+    "first": "ML L:0-128 mv:64-128 SC SD ma:0-64 L:128-256 ma:128-192 c:64-128 IC PC F:0-128 xa:64-96 F:128-256 xa:0-32 xa:128-160 xa:192-224 xv:96-128 xv:32-64 S:0-128 xv:224-256 c:0-64 xv:160-192 c:128-192 sv:192-224 ma:192-256 c:192-256 S:128-256 lv O D0 sa:96-128 na sa:224-256 Vm p y:0-2 y:2-4 y:4-6 ev sa:32-64 U y:6-8 t:224-256 y:8-10 y:10-12 y:12-14 sa:64-96 t:192-224 t:64-128 u:0 u:9 u:1 u:2 y:14-16 h0 u:3 h u:4 u:5 u:6 hj u:7 fw u:8 hm at nw fr sa:0-32 t:0-64 Z:0-128 sa:128-192 t:128-192 Z:128-256 R:0-128 R:128-256 Rm tm l1 L+ tt1 ch pa ca ob cl bo mg ML+ oc ma+:0-64 ma+:128-192 mv+:64-128 ps",
+    "mid": "D0 F:0-128 xa:0-32 xa:64-96 F:128-256 xa:128-160 xa:192-224 xv:96-128 xv:32-64 S:0-128 xv:160-192 xv:224-256 S:128-256 c:64-128 sv:192-224 c:0-64 t:192-224 O lv Vm sa:96-128 ma:224-256 sa:224-256 y:0-2 y:2-4 c:128-192 y:4-6 ma:192-224 na ea y:6-8 y:8-10 U c:192-256 y:10-12 p t:224-256 y:12-14 u:0 y:14-16 u:1 u:9 sa:64-96 u:2 h t:64-128 u:3 at h0 hj u:5 hm u:4 u:7 fw u:6 nw fr sa:0-32 u:8 sa:32-64 t:0-64 Z:0-128 sa:128-192 t:128-192 tm l1 R:0-128 ca R:128-256 Z:128-256 Rm tt1 L+ ch pa bo ob cl mg ma+:0-64 mv+:64-128 ps oc ML+ ma+:128-192",
+    "last": "F:0-128 F:128-256 xv:96-128 xv:32-64 xa:64-96 xa:0-32 S:0-128 xv:160-192 xv:224-256 sv:192-224 c:0-64 c:64-128 t:192-224 xa:192-224 xa:128-160 S:128-256 D0 O lv Vm na ma:192-224 ma:224-256 sa:224-256 y:0-2 y:2-4 ea U y:4-6 c:128-192 y:6-8 c:192-256 y:8-10 u:9 u:0 p y:10-12 y:12-14 u:1 y:14-16 u:5 h u:7 t:224-256 u:8 fw hj at h0 nw hm fr sa:0-32 sa:64-96 sa:32-64 sa:96-128 t:64-128 t:0-64 Z:0-128 sa:128-192 t:128-192 Z:128-256 u:2 u:3 u:4 u:6 tm l1 R:0-128 R:128-256 pa wr:512-1024 bo Rm tt1 ch ws:512-1024 ca cl wr:0-512 ws:0-512 mg om ps op",
 }
+PLAN = {
+    "first": "L:0-128 EN ML ma:0-64 mv:64-128 L:128-256 G0 G:0-128 F:128-256 mv:192-256 IC F:0-128 nv sp:1-3 ma:128-192 G:128-256 SC xa:96-128 xv:64-96 S:64-128 xa:0-32 xv:32-64 S:0-64 xa:128-160 xv:160-192 S:128-192 xv:224-256 PC xa:192-224 S:192-256 O y:0-2 y:2-4 sa:128-160 SD la Vm sa:0-64 y:4-6 ea sa:160-224 y:6-8 y:8-10 y:10-12 y:12-14 y:14-16 t:0-32 U sv:96-128 fv t:128-160 t:96-128 D0 u:0 u:9 h0 new fr G0+ u:1 hi hm u:2 u:5 u:3 u:7 u:4 sa:64-96 t:64-96 u:6 t:160-192 sa:224-256 tm u:8 l1 sp:0-1 t:32-64 R:0-128 at Z:0-128 t:192-224 t:224-256 R:128-256 Z:128-256 Rm cm tt1 L+ ch sp:6-8 cl pa ob oc bo mg mv+:128-192 G+:128-192 sp:3-6 ma+:0-64 G+:0-64 ma+:64-128 G+:64-128 sp:8-9 ps ML+ nv+",
+    "mid": "D0 F:0-128 xa:0-32 F:128-256 xv:32-64 xv:96-128 xa:64-96 S:0-64 S:64-128 xv:160-192 xa:128-160 S:128-192 xa:192-224 xv:224-256 S:192-256 mv:192-256 G:192-256 O y:0-2 sa:0-64 la Vm y:2-4 y:4-6 t:0-32 y:6-8 sa:64-96 t:64-96 y:8-10 y:10-12 y:12-14 y:14-16 t:32-64 sa:128-160 ea sa:96-128 U sa:160-224 fv t:96-128 sa:224-256 u:0 u:9 u:1 new fr u:2 u:5 hi u:3 at t:128-160 u:4 u:7 u:6 t:160-192 h0 hm tm u:8 l1 Z:0-128 G0+ R:0-128 t:192-224 t:224-256 Z:128-256 R:128-256 Rm ob L+ cm tt1 oc ch pa cl bo mg mv+:128-192 G+:128-192 ma+:0-64 G+:0-64 ma+:64-128 ps nv+ ML+ G+:64-128",
+    "last": "F:0-128 F:128-256 xv:32-64 xa:0-32 S:0-64 xa:64-96 xv:96-128 S:64-128 xv:160-192 xa:128-160 S:128-192 xa:192-224 xv:224-256 S:192-256 mv:192-256 G:192-256 O y:0-2 lv sa:96-128 sa:128-160 sa:64-96 sa:0-64 y:2-4 Vm y:4-6 y:6-8 y:8-10 y:10-12 y:12-14 t:64-96 y:14-16 t:32-64 t:96-128 t:128-160 ea U fv t:0-32 D0 at Z:0-128 sa:224-256 t:224-256 u:0 u:1 u:9 h0 u:5 new fr u:7 sa:160-224 t:192-224 u:8 t:160-192 Z:128-256 R:0-128 u:2 hi u:3 wv:0-512 u:4 wv:512-1024 u:6 dc:0-512 hm tm R:128-256 Rm tt1 l1 dc:512-1024 ch ws:512-1024 ws:0-512 da:0-512 dr:0-512 pa da:512-1024 bo dc:1024-1536 dr:512-1024 ps op da:1024-1536 dr:1024-1536 cl mg om",
+}
+TRACE = []
 
 
 def rank_program(g, core, T, topo):
@@ -82,6 +80,7 @@ def rank_program(g, core, T, topo):
 
     def emit(q, call, reads, writes, own=None):
         reads = list(reads) + [a[5] for a in list(reads) + list(writes) if len(a) > 5]
+        TRACE.append((q, [a[1:4] for a in reads], [a[1:4] for a in writes]))
         need = {}
         for a, wr in [(a, False) for a in reads] + [(a, True) for a in writes]:
             psum = SCRATCH[a[1]][0] == "psum"
@@ -126,6 +125,9 @@ def rank_program(g, core, T, topo):
         else:
             emit("v", lambda: g.vector.tensor_scalar(out[0], a[0], val(s1), val(s2), op0, op1), [a] + col(s1) + col(s2), [out])
 
+    def scan(out, d0, d1, op0, op1):
+        emit("v", lambda: g.vector.tensor_tensor_scan(out[0], d0[0], d1[0], 0.0, op0, op1), [d0, d1], [out])
+
     def fill(out, c):
         emit("v", lambda: g.vector.memset(out[0], c), [], [out])
 
@@ -138,6 +140,14 @@ def rank_program(g, core, T, topo):
         else:
             emit("a", lambda: g.scalar.activation(out[0], a[0], fn, bias=val(bias), scale=scale, accum_out=acc[0]),
                  [a] + col(bias), [out, acc])
+
+    def move(e, out, a, scale=1.0, bias=0.0):
+        if scale == 1.0 and bias == 0.0:
+            (act if e == "a" else cp)(out, a)
+        elif e == "a":
+            act(out, a, bias, scale)
+        else:
+            ts(out, a, scale, Op.mult, bias, Op.add)
 
     def mm(out, lhs, rhs, start, stop):
         emit("t", lambda: g.tensor.matmul(out[0], lhs[0], rhs[0], start, stop), [lhs, rhs], [out])
@@ -179,7 +189,7 @@ def rank_program(g, core, T, topo):
         expect(A("L1R", t * 16, (t + 1) * 16), source(t), "a1%d" % t)
         expect(A("CHR", t * L, (t + 1) * L), source(t), "a2%d" % t)
 
-    load("s", A("M", 0, V), T.mk[:], "d_mk")
+    load("s", A("MK"), T.mk[:], "d_mk")
     load("s", A("SU", 0, V // 2), T.su[:, 0:V // 2], "d_su")
     load("s", A("SU", V // 2, V), T.su[:, V // 2:V], "d_su2")
     load("s", A("PL"), T.pl[:], "d_pl")
@@ -191,42 +201,29 @@ def rank_program(g, core, T, topo):
     load("s", A("X", W, WX), T.xf[:, 0:WX - W], "d_xe")
     load("s", A("ST", W, WX), T.stp[:, 0:WX - W], "d_se")
 
-    def send_levels(t):
-        after = [A("CHR", (t - 1) * L, t * L)] if t else []
-        send(A("M", 0, V), source(t), A("MR", t * VX, t * VX + V), "am%d" % t, "lm", after)
-
     iota(A("ip", 0, 1), [[0, 1]], 1, False)
     iota(A("ion"), [[1, 144]], 0)
     iota(A("iog"), [[1, 8], [0, 16]], 0)
     iota(A("io16"), [[1, 16]], 0)
-    iota(A("seg"), [[0, 96], [15, 16]], 0)
-    send_levels(0)
     ip = A("ip", 0, 1)
-
-    def KI(k):
-        return A("KI", k, k + 1)
-
-    def KF(k):
-        return A("KF", k, k + 1)
-
-    def KD(k):
-        return A("KD", k, k + 1)
 
     def MAT(k):
         return A("MAT", 128 * k, 128 * (k + 1))
 
-    fill(A("M", V, VX), 0.0)
-    for t in range(RO):
-        act(A("MR", t * VX + V, (t + 1) * VX), A("M", V, VX))
-    act(A("P", V, VX), A("M", V, VX))
-    ts(KI(0), ip, 127, Op.bitwise_and)
-    ts(KI(1), ip, 15, Op.bitwise_and)
-    ts(KI(2), ip, 112, Op.bitwise_and)
-    ts(KI(3), ip, 16, Op.bitwise_and)
-    ts(KI(4), ip, 4, Op.arith_shift_right)
+    ONE, NEG, NIL, FALL, TOP = [MAT(k) for k in (0, 1, 10, 11, 12)]
+    SORT = [[2, 5], [4, 3]]
+
+    def encode(out, a):
+        act(out, a, LOW * LN2, BITS * LN2, Fn.Exp)
+
+    fill(A("zero"), 0.0)
+    encode(A("M", V, VX), A("zero"))
+    for k, (c, op) in enumerate([(127, Op.bitwise_and), (15, Op.bitwise_and), (112, Op.bitwise_and), (16, Op.bitwise_and),
+                                 (4, Op.arith_shift_right)]):
+        ts(A("KI", k, k + 1), ip, c, op)
     cp(A("KF", 0, 5), A("KI", 0, 5))
-    kp, kr, kg, kh, kgi = [KF(k) for k in range(5)]
-    gE, hs, psw, wt, m0, m1, jb0, jb1 = [KD(k) for k in range(8)]
+    kp, kr, kg, kh, kgi = [A("KF", k, k + 1) for k in range(5)]
+    gE, hs, psw, wt, m0, m1 = [A("KD", k, k + 1) for k in range(6)]
     ts(gE, kg, 15.0, Op.add)
     ts(hs, kh, -2.0, Op.mult, 16.0, Op.add)
     ts(wt, kr, 2.0, Op.mult, 1.0, Op.add)
@@ -234,316 +231,228 @@ def rank_program(g, core, T, topo):
     ts(m0, kh, -1.0 / 16, Op.mult, 1.0, Op.add)
     ts(psw, hs, kp, Op.add)
     i128 = A("ion", 0, 128)
-    ts(MAT(0), i128, kp, Op.is_equal)
-    ts(MAT(1), i128, psw, Op.is_equal)
+    ts(ONE, i128, kp, Op.is_equal)
     ts(A("WE"), A("ion"), gE, Op.is_equal)
     for k, (tg, mk) in enumerate([(kp, m0), (kp, m1), (psw, m1), (psw, m0)]):
         ts(MAT(2 + k), i128, tg, Op.is_equal, mk, Op.mult)
-    ts(MAT(10), A("iog"), kgi, Op.is_equal)
-    ts(A("pq", 16, 32), A("io16"), 16.0, Op.mult, kr, Op.add)
-    ts(A("dl"), A("pq", 16, 32), -1.0 / 2048, Op.mult)
+    ts(A("BH"), A("iog"), kgi, Op.is_equal, 0.5, Op.mult)
+    ts(A("li"), A("io16"), 16.0, Op.mult, kr, Op.add)
+    ts(A("dl", 0, 16), A("li"), -1.0 / 2048, Op.mult)
+    ts(A("jb"), A("li"), 16.0, Op.mult)
+    fill(A("ht"), 0.0)
+    ts(FALL, i128, kp, Op.is_equal, DOWN, Op.mult)
+    fill(NIL, 0.0)
+
+    def spare(k):
+        if k < RO:
+            act(A("MR", k * VX + V, (k + 1) * VX), A("M", V, VX))
+        else:
+            act(A(("low", "P", "MO")[k - RO], *((0, L), (V, VX), (V, VX))[k - RO]), A("M", V, VX))
 
     def scaled_constants():
-        act(A("WH"), A("WE"), 0.0, 0.5)
-        act(A("IF"), MAT(0))
+        act(NEG, ONE, 0.0, -1.0)
+        act(A("IF"), ONE)
         act(A("WW"), A("WE"), 0.0, wt)
-        act(jb0, kr, kh, 32.0)
-        act(MAT(11), MAT(0), 0.0, 0.0)
-        act(jb1, jb0, hs)
-        act(A("jb", 8, 16), A("io16", 0, 8), jb0, 512.0)
-        act(A("jb", 0, 8), A("io16", 0, 8), jb1, 512.0)
+        act(A("WN"), A("WE"), 0.0, -1.0)
+        act(TOP, ONE, 0.0, HALF_TOP)
 
     def step_constants():
         for k in range(4):
             act(MAT(6 + k), MAT(2 + k), 0.0, -1.0)
 
-    def pack_constants():
-        fh, gZ, r8, r9, ct = [KD(k) for k in range(8, 13)]
-        ts(fh, kr, 8.0, Op.is_ge, 8.0, Op.mult)
-        ts(A("WL"), A("ion"), gE, Op.is_equal)
-        ts(gZ, fh, gE, Op.add)
-        ts(r8, fh, -1.0, Op.mult, kp, Op.add)
-        ts(ct, fh, -4386.0, Op.mult, 34816.0, Op.add)
-        ts(A("WZ"), A("ion"), gZ, Op.is_equal)
-        ts(r9, r8, 8.0, Op.add)
-        ts(A("kk", 128, 256), i128, r8, Op.is_equal, -128.0, Op.mult)
-        ts(A("kk", 0, 128), i128, r9, Op.is_equal)
-        act(A("CT"), A("M", V, VX), ct)
-        act(MAT(12), MAT(0), 0.0, 128.0)
-        tt(MAT(13), A("kk", 128, 256), A("kk", 0, 128), Op.add)
-
-    def PU(lo, hi):
-        return A("pZ", L + lo, L + hi) if PLAN["pack"] else A("pU", lo, hi)
-
     def input_constants():
         ts(A("hc"), A("HP"), -1.0 / 2048, Op.mult, 0.5, Op.add)
         cp(A("thf", 0, RO), A("TH", 0, RO))
-        cp(A("capa", 0, 1), A("CP", 0, 1))
-        tt(A("hd", 0, 16), A("hc", 16, 32), A("hc", 0, 16), Op.subtract)
-        tt(A("rr"), A("hc", 48, 64), A("hc", 32, 48), Op.subtract)
-        tt(A("he", 16, 32), A("hc", 32, 48), A("hc", 0, 16), Op.subtract)
-        tt(A("hd", 16, 32), A("rr"), A("hd", 0, 16), Op.subtract)
-
-    def scaled_inputs():
-        act(A("he", 0, 16), A("hc", 0, 16), 8.0)
-        act(A("th2", 16, 16 + RO), A("thf", 0, RO), 0.5, -1.0)
-        act(A("th2", 0, RO), A("thf", 0, RO), 0.0, 0.5)
-        act(A("th2", 8, 8 + RO), A("thf", 0, RO), 0.0, -0.5)
-        act(A("cpf", 0, 1), A("capa", 0, 1), 1088.0)
-
-    def su_list(q, lo, hi):
-        cp(A("SL", q * L + lo, q * L + hi), A("SU", 4 * lo + q, 4 * hi, 4))
-
-    def gm_piece(e, t, lo, hi):
-        q = t % 4
-        src = IND(A("M", 0, V), A("SL", q * L + lo, q * L + hi))
-        if e == "a":
-            act(A("gm", 16 * lo, 16 * hi), src, -4.0)
-        else:
-            ts(A("gm", 16 * lo, 16 * hi), src, -4.0, Op.add)
-
-    def scan(lo, hi):
-        o, d0, d1 = A("sc", 16 * lo, 16 * hi), A("seg", 0, 16 * (hi - lo)), A("gm", 16 * lo, 16 * hi)
-        emit("v", lambda: g.vector.tensor_tensor_scan(o[0], d0[0], d1[0], 0.0, Op.min, Op.max), [d0, d1], [o])
+        ts(A("cpf", 0, 1), A("CP", 0, 1), 1216.0, Op.add)
+        fill(A("rem", 0, 1), -1216.0)
+        for k in range(3):
+            tt(A("hd", k, 64, 4), A("hc", 48 - 16 * k, 64 - 16 * k), A("hc", 32 - 16 * k, 48 - 16 * k), Op.subtract)
+        ts(A("hd", 3, 64, 4), A("hc", 0, 16), 256.0, Op.add)
 
     def E(name, r):
         return A(name, 15 - r, 143 - r)
 
-    def old_levels(t):
-        act(A("nold"), A("M", t % 4, V, 4), 7.5, -1.0, Fn.Sign)
-        mm(A("pC", 0, 16), MAT(0), A("dl"), True, False)
-        for r in range(16):
-            mm(A("pC", 0, 16), E("WH", r), A("nold", r, L, 16), False, False)
+    small = [
+        lambda: cp(A("ui"), A("pU", 0, 32)),
+        lambda: ts(A("uw"), A("ui"), 63, Op.bitwise_and),
+        lambda: ts(A("ht", 1, 64, 4), A("uw", 16, 32), 48.0, Op.is_ge),
+        lambda: ts(A("ht", 2, 64, 4), A("uw", 16, 32), 32.0, Op.is_ge),
+        lambda: ts(A("ht", 3, 64, 4), A("uw", 16, 32), 16.0, Op.is_ge),
+        lambda: ts(A("jm"), A("uw", 0, 16), 0.25, Op.mult, 1.0, Op.max),
+        lambda: scan(A("hs"), A("ht"), A("hd"), Op.mult, Op.add),
+        lambda: tt(A("ja"), A("jm"), A("jb"), Op.add),
+        lambda: cp(A("jl"), A("ja")),
+        lambda: cp(A("dl", 16, 32), A("pU", 32, 48)),
+    ]
+
+    def step(n, t, lo, hi):
+        q = t % 4
+        wx = W if t == 0 else WX
+        last = t == RO - 1
+        lanesM, lanesP, lanesO = A("M", q, V, 4), A("P", q, V, 4), A("MO", q, V, 4)
+        back = A("NEW", RO * L, (RO + 1) * L)
+        new, l1, ch = A("NEW", t * L, (t + 1) * L), A("L1", t * 16, (t + 1) * 16), A("CH", t * L, (t + 1) * L)
+        l1r = A("L1R", t * 16, (t + 1) * 16)
+        th = A("thf", t, t + 1)
+        wide = (16 * lo, 16 * hi)
+        if n == "F":
+            cp(A("offs", lo, hi), A("P" if t else "PL", 4 * lo + q, 4 * hi, 4))
+        elif n == "L":
+            if t < 4:
+                cp(A("SL", q * L + lo, q * L + hi), A("SU", 4 * lo + q, 4 * hi, 4))
+        elif n in ("xa", "xv"):
+            move(n[1], A("xk", *wide), IND(A("X", 0, wx), A("offs", lo, hi)), -1.0)
+        elif n in ("sa", "sv"):
+            move(n[1], A("sk", *wide), IND(A("ST", 0, wx), A("offs", lo, hi)))
+        elif n in ("ma", "mv"):
+            move(n[1], A("gm", *wide), IND(A("M", 0, V), A("SL", q * L + lo, q * L + hi)))
+        elif n == "G0":
+            mm(A("pG", 0, L), NIL, A("zero"), True, False)
+        elif n == "G":
+            for k in range(16):
+                mm(A("pG", lo, hi), FALL, A("gm", 16 * lo + k, 16 * hi, 16), False, False)
+        elif n == "nv":
+            ts(A("SS", 2 * L, 3 * L), lanesM, HIGH, Op.is_lt)
+        elif n == "S":
+            for a in range(16):
+                mm(A("pS", lo, hi), NEG, A("xk", 16 * lo + a, 16 * hi, 16), a == 0, a == 15)
+        elif n in ("la", "lv"):
+            move(n[1], A("SS", L, 2 * L), A("pS", 0, L))
+        elif n == "O":
+            ts(A("ov"), A("pS", 0, L), A("cpf", 0, 1), Op.subtract, A("rem", 0, 1), Op.is_gt)
+        elif n == "y":
+            for a in range(lo, hi):
+                ya = A("y", a * L, (a + 1) * L)
+                scan(ya, A("ov"), A("xk", a, 16 * L, 16), Op.max, Op.mult)
+                mm(A("pL", 0, L), E("WN", a), ya, a == 0, a == 15)
+        elif n == "fv":
+            ts(A("f15"), A("pL", 0, L), th, Op.is_ge, HALF_TOP, Op.mult)
+            mm(A("pG", 0, L), TOP, A("f15"), False, True)
+        elif n == "new":
+            tt(new, A("pG", 0, L), lanesM, Op.max)
+        elif n == "hi":
+            ts(A("hi"), new, HIGH, Op.is_ge)
+        elif n == "fr":
+            send(new, source(t), A("FR", t * L, (t + 1) * L), "an%d" % t, "ln")
+        elif n in ("cm", "ca"):
+            move("v" if n == "cm" else "a", lanesM, new)
+        elif n == "Vm":
+            for h in range(2):
+                for x in range(2):
+                    mm(A("pS", L + h, 2 * L, 2), MAT(SORT[h][x]), A("SS", L + x, 2 * L, 2), x == 0, x == 1)
+        elif n in ("ea", "ev"):
+            move(n[1], A("SS", 0, L), A("pS", L, 2 * L), 4.0)
+        elif n == "U":
+            for r in range(16):
+                mm(A("pU", 0, 48), E("WW", r), A("SS", r, 3 * L, 16), r == 0, r == 15)
+        elif n == "u":
+            small[lo]()
+        elif n == "h0":
+            mm(A("pC", 0, 16), ONE, A("dl", 0, 16), True, False)
+            mm(A("pC", 0, 16), ONE, A("dl", 16, 32), False, False)
+        elif n == "hm":
+            for r in range(16):
+                mm(A("pC", 0, 16), E("WW", r), A("hi", r, L, 16), False, r == 15)
+        elif n == "tm":
+            tt(A("tm"), A("pC", 0, 16), A("hs", 3, 64, 4), Op.min)
+        elif n == "l1":
+            ts(l1, A("tm"), -2048.0, Op.mult, float(V + 256 * 2048), Op.add)
+            send(l1, dest(t), l1r, "a1%d" % t, "l1")
+        elif n == "ob":
+            act(A("ob"), A("tm"), -256.0 - 1.0 / 4096, 1.0, Fn.Sign, A("af", 0, 1))
+            mm(A("pA", 0, 1), A("BH"), A("af", 0, 1), True, True)
+            act(A("ak", 0, 1), A("pA", 0, 1), 151.5625, 0.125)
+        elif n == "oc":
+            ts(A("rem", 0, 1), A("ak", 0, 1), -8.0, Op.mult, A("pA", 0, 1), Op.add)
+        elif n == "t":
+            o, i = A("skT", *wide), A("sk", *wide)
+            emit("v", lambda: g.vector.transpose(o[0], i[0]), [i], [o])
+        elif n == "D0":
+            mm(A("pD", 0, L), NIL, A("zero"), True, False)
+        elif n == "at":
+            mm(A("pZ", 0, L), A("IF"), lanesP, True, False)
+        elif n == "Z":
+            for bank, m in (("pD", 4), ("pZ", 0)):
+                for x in range(2):
+                    for h in range(2):
+                        mm(A(bank, lo + x, hi, 2), MAT(m + SORT[x][h]), A("skT", 16 * lo + 16 * h, 16 * hi, 32), False, False)
+        elif n == "R":
+            act(A("R", lo, hi), IND(A("skT", 0, 16 * hi), A("jl", lo // 16, hi // 16)))
+        elif n == "Rm":
+            for x in range(2):
+                for h in range(2):
+                    mm(A("pD", x, L, 2), MAT(SORT[x][h]), A("R", h, L, 2), False, x + h == 2)
+        elif n == "tt1":
+            tt(A("tt1"), A("hi"), A("pD", 0, L), Op.mult)
+            mm(A("pZ", 0, L), ONE, A("tt1"), False, True)
+        elif n == "ch":
+            if t == RO - 1:
+                ts(A("t2"), A("pZ", 0, L), float(W), Op.is_ge, -float(W), Op.mult)
+                tt(A("t3"), A("pZ", 0, L), A("t2"), Op.add)
+                cp(ch, A("t3"))
+            else:
+                cp(ch, A("pZ", 0, L))
+            send(ch, dest(t), A("CHR", t * L, (t + 1) * L), "a2%d" % t, "l2")
+        elif n in ("pv", "pa"):
+            move(n[1], A("MR", t * VX + q, t * VX + V, 4), A("FR", t * L, (t + 1) * L))
+        elif n == "bo":
+            move("a", back, IND(A("MR", t * VX, (t + 1) * VX), l1), DOWN)
+        elif n == "cl":
+            cp(IND(A("MO" if last else "M"), l1r), A("zero" if last else "low"))
+        elif n == "mg":
+            if last:
+                tt(lanesO, lanesO, A("bk"), Op.max)
+            else:
+                tt(lanesM, lanesM, back, Op.max)
+        elif n == "ML":
+            after = [A("CHR", (t - 1) * L, t * L)] if t else []
+            send(A("M", 0, V), source(t), A("MR", t * VX, t * VX + V), "am%d" % t, "lm", after)
+        elif n == "ps":
+            cp(IND(A("P"), l1r), A("CHR", t * L, (t + 1) * L))
+        elif n == "PC":
+            cp(A("P", 0, V), A("PL"))
+        elif n == "sp":
+            for k in range(lo, hi):
+                spare(k)
+        elif n == "EN":
+            encode(A("M", 0, V), A("MK"))
+        elif n in ("dc", "da", "dr"):
+            coded = A("M", lo, hi) if lo < V else A("NEW", t * L, (t + 2) * L)
+            bank = A(("pS", "pA", "pU")[lo // 512])
+            if n == "dc":
+                ts(A("dc", lo, hi), coded, HIGH, Op.min, ZERO, Op.max)
+            elif n == "da":
+                act(A("dh", lo, hi), coded, 2.0 ** -50, 2.0 ** -75, Fn.Ln)
+                act(A("dw", lo, hi), A("dc", lo, hi), 0.0, 2.0 ** 30, Fn.Ln)
+                mm(bank, ONE, A("dh", lo, hi), True, False)
+                mm(bank, ONE, A("dw", lo, hi), False, True)
+            else:
+                ts(A("dr", lo, hi), bank, 1.0 / (BITS * LN2), Op.mult, 136.0 + (20 - LOW - 6.2) / BITS, Op.add)
+                if lo < V:
+                    ts(A("MO", lo, hi), A("dr", lo, hi), -136.0, Op.add)
+                else:
+                    ts(lanesO, A("dr", V, V + L), -136.0, Op.add)
+                    ts(A("bk"), A("dr", V + L, V + 2 * L), -136.0, Op.add)
+        elif n == "wv":
+            ts(A(("pL", "pG")[lo // 512]), A("P", lo, hi), float(W), Op.is_ge, -float(W), Op.mult)
+        elif n == "ws":
+            tt(A("P", lo, hi), A(("pL", "pG")[lo // 512]), A("P", lo, hi), Op.add)
+        elif n == "om":
+            store("s", T.ymk[:], A("MO", 0, V), "d_om")
+        elif n == "op":
+            store("s", T.ypl[:], A("P", 0, V), "d_op")
+        else:
+            {"SC": scaled_constants, "SD": step_constants, "IC": input_constants}[n]()
+
+    def run(script, t):
+        for word in script.split():
+            TRACE.append(word)
+            n, _c, span = word.partition(":")
+            lo, hi = ([int(v) for v in span.split("-")] + [0])[:2] if span else (0, L)
+            step(n.rstrip("+"), t + n.endswith("+"), lo, hi)
 
     for t in range(RO):
-        q = t % 4
-        last = t == RO - 1
-        wx = W if t == 0 else WX
-        lanesM, lanesP = A("M", q, V, 4), A("P", q, V, 4)
-        th = A("thf", t, t + 1)
-        new = A("NEW", t * L, (t + 1) * L)
-        l1 = A("L1", t * 16, (t + 1) * 16)
-
-        def turn(lo, hi):
-            o, i = A("skT", 16 * lo, 16 * hi), A("sk", 16 * lo, 16 * hi)
-            emit("v", lambda: g.vector.transpose(o[0], i[0]), [i], [o])
-
-        small = [
-            lambda: cp(A("ui", 16, 32), PU(16, 32)),
-            lambda: ts(A("b0", 0, 16), A("ui", 16, 32), 4, Op.arith_shift_right, 1, Op.bitwise_and),
-            lambda: ts(A("b0", 16, 32), A("ui", 16, 32), 4, Op.arith_shift_right, 1, Op.bitwise_and),
-            lambda: ts(A("b1"), A("ui", 16, 32), 5, Op.arith_shift_right, 1, Op.bitwise_and),
-            lambda: tt(A("pq"), A("b0"), A("hd"), Op.mult),
-            lambda: ts(A("jj"), A("ui", 0, 16), 15, Op.bitwise_and),
-            lambda: tt(A("pr"), A("pq"), A("he"), Op.add),
-            lambda: ts(A("jm"), A("jj"), 1.0, Op.max),
-            lambda: tt(A("rr"), A("b1"), A("pr", 16, 32), Op.mult),
-            lambda: tt(A("ja"), A("jm"), A("jb"), Op.add),
-            lambda: tt(A("cc"), A("rr"), A("pr", 0, 16), Op.add),
-            lambda: cp(A("jl"), A("ja")),
-            lambda: cp(A("ui", 0, 16), PU(0, 16)),
-        ]
-        def sums(lo, hi):
-            return A("pS" if lo < PLAN["split"] else "pA", lo, hi)
-
-        def pair(a, lo, hi):
-            return A(("pO", "pA", "pU", "pD")[a // 2], a % 2 * L + lo, a % 2 * L + hi)
-
-        done = [0]
-
-        def burden(a, lo, hi):
-            mm(A("pL", lo, hi), E("WE", a), A("y", a * L + lo, a * L + hi), done[0] % 16 == 0, done[0] % 16 == 15)
-            done[0] += 1
-
-        def items(script, tm=t):
-            for word in script.split():
-                part = word.split(":")
-                n = part[0]
-                lo, hi = [int(v) for v in part[1].split("-")] if len(part) > 1 else (0, L)
-                if n == "xa":
-                    act(A("xk", 16 * lo, 16 * hi), IND(A("X", 0, wx), A("offs", lo, hi)))
-                elif n == "xv":
-                    cp(A("xk", 16 * lo, 16 * hi), IND(A("X", 0, wx), A("offs", lo, hi)))
-                elif n == "sa":
-                    act(A("sk", 16 * lo, 16 * hi), IND(A("ST", 0, wx), A("offs", lo, hi)))
-                elif n == "sv":
-                    cp(A("sk", 16 * lo, 16 * hi), IND(A("ST", 0, wx), A("offs", lo, hi)))
-                elif n in ("ma", "mv"):
-                    gm_piece(n[1], tm, lo, hi)
-                elif n == "c":
-                    scan(lo, hi)
-                elif n == "S":
-                    for a in range(16):
-                        mm(sums(lo, hi), MAT(0), A("xk", 16 * lo + a, 16 * hi, 16), a == 0, a == 15)
-                elif n == "O":
-                    ts(A("pO", lo, hi), sums(lo, hi), A("capa", 0, 1), Op.is_gt)
-                elif n == "B":
-                    act(A("Sb", lo, hi), sums(lo, hi))
-                elif n == "y":
-                    a0, a1 = [int(v) for v in part[-1].split("-")]
-                    if len(part) == 2:
-                        lo, hi = 0, L
-                    for a in range(a0, a1):
-                        ya = A("y", a * L + lo, a * L + hi)
-                        tt(ya, A("xk", 16 * lo + a, 16 * hi, 16), A("pO", lo, hi), Op.mult)
-                        burden(a, lo, hi)
-                elif n == "K":
-                    for a in range(8):
-                        mm(pair(a, lo, hi), MAT(0), A("xk", 16 * lo + a, 16 * hi, 16), True, False)
-                        mm(pair(a, lo, hi), MAT(12), A("xk", 16 * lo + a + 8, 16 * hi, 16), False, True)
-                elif n == "Bv":
-                    cp(A("Sb"), A("pS", 0, L))
-                elif n == "Os":
-                    ts(A("ov"), A("Sb"), A("capa", 0, 1), Op.is_gt)
-                elif n == "C0":
-                    mm(A("pL", 0, L), MAT(0), A("CT"), True, False)
-                elif n == "w":
-                    for a in range(lo, hi):
-                        ya = A("yh", a * L, (a + 1) * L)
-                        tt(ya, pair(a, 0, L), A("ov"), Op.mult)
-                        mm(A("pS", L, 2 * L), E("WZ", a), ya, done[0] == 0, done[0] == 7)
-                        mm(A("pL", 0, L), E("WL", a), ya, False, False)
-                        done[0] += 1
-                elif n == "k":
-                    ts(A("kk"), A("pS", L, 2 * L), 1.0 / 128, Op.mult, 136.0 - 63.5 / 128, Op.add)
-                    mm(A("pL", 0, L), MAT(13), A("kk"), False, True)
-                elif n == "KC":
-                    pack_constants()
-                elif n == "R":
-                    got = [A("R", 128 - 128 * x + lo // 2, 128 - 128 * x + hi // 2) for x in range(2)]
-                    if hi - lo == L:
-                        act(A("R"), IND(A("skT"), A("jl")))
-                    else:
-                        for x in range(2):
-                            act(got[x], IND(A("skT", 0, 16 * hi), A("jl", 8 - 8 * x + lo // 32, 8 - 8 * x + hi // 32)))
-                    for x in range(2):
-                        for h in range(2):
-                            mm(A("pD", lo + (h ^ x), hi, 2), MAT(2 + 2 * x + h), got[x], False, hi == L and x + h == 2)
-                elif n == "D0":
-                    mm(A("pD", 0, L), MAT(11), A("seg", 0, L), True, False)
-                elif n == "U":
-                    for r in range(16):
-                        mm(PU(16, 32), E("WW", r), A("Sb", r, L, 16), r == 0, r == 15)
-                elif n == "V":
-                    for r in range(16):
-                        mm(PU(0, 16), E("WW", r), A("Sm", r, L, 16), r == 0, r == 15)
-                elif n == "Vm":
-                    for x in range(2):
-                        for c in range(2):
-                            mm(A("pA", L + 128 - 128 * x, 2 * L - 128 * x), MAT(2 + 2 * x + c), A("Sb", c, L, 2), c == 0, c == 1)
-                elif n == "Ve":
-                    act(A("Sm"), A("pA", L, 2 * L))
-                elif n == "ha":
-                    act(A("sg"), A("pre"), -7.5, 1.0, Fn.Sign)
-                    act(A("thp"), A("sg"), A("th2", t, t + 1), A("th2", 8 + t, 9 + t))
-                elif n == "p":
-                    tt(A("pre"), A("sc", 15, 4096, 16), lanesM, Op.max)
-                elif n == "h":
-                    ts(A("thp"), A("pre"), 8.0, Op.is_lt, th, Op.mult)
-                elif n == "t":
-                    turn(lo, hi)
-                elif n == "u":
-                    for step in small[lo:hi]:
-                        step()
-                elif n == "Z":
-                    for bank, m in (("pD", 6), ("pZ", 2)):
-                        for x in range(2):
-                            for h in range(2):
-                                mm(A(bank, lo + (h ^ x), hi, 2), MAT(m + 2 * x + h),
-                                   A("skT", 16 * lo + 16 * h, 16 * hi, 32), False, False)
-                elif n == "fv":
-                    ts(A("f15"), A("pL", 0, L), th, Op.is_ge, 15.0, Op.mult)
-                elif n == "fa":
-                    act(A("sg"), A("pL", 0, L), A("th2", 16 + t, 17 + t), 1.0, Fn.Sign)
-                    act(A("f15"), A("sg"), 7.5, 7.5)
-                elif n == "new":
-                    tt(new, A("f15"), A("pre"), Op.max)
-                    send(new, source(t), A("FR", t * L, (t + 1) * L), "an%d" % t, "ln")
-                    act(lanesM, new)
-                elif n == "tm":
-                    tt(A("tm"), A("pC", 0, 16), A("cc"), Op.min)
-                elif n == "l1":
-                    ts(l1, A("tm"), -2048.0, Op.mult, float(V + 8 * 2048), Op.add)
-                    send(l1, dest(t), A("L1R", t * 16, (t + 1) * 16), "a1%d" % t, "l1")
-                elif n == "ob" and not last:
-                    act(A("ob"), A("tm"), -8.0 - 1.0 / 4096, 1.0, Fn.Sign)
-                    mm(A("pA", 0, 16), MAT(10), A("ob"), True, True)
-                    items("A")
-                elif n == "n":
-                    old_levels(tm)
-                elif n == "A":
-                    act(A("aw"), A("pA", 0, 16), 8.0, 0.5, Fn.Identity, A("af", 0, 1))
-                    act(A("ak", 0, 1), A("af", 0, 1), 135.5625, 0.125)
-                    act(A("af", 2, 3), A("af", 0, 1), A("cpf", 0, 1))
-                    act(A("capa", 0, 1), A("ak", 0, 1), A("af", 2, 3), -8.0)
-                elif n == "F":
-                    cp(A("offs"), lanesP if t else A("PL", 0, V, 4))
-                elif n == "at":
-                    mm(A("pZ", 0, L), A("IF"), lanesP, True, False)
-                elif n == "PC":
-                    cp(A("P", 0, V), A("PL"))
-                elif n == "L":
-                    su_list(tm % 4, lo, hi)
-                elif n == "SC":
-                    scaled_constants()
-                elif n == "SD":
-                    step_constants()
-                elif n == "IC":
-                    input_constants()
-                elif n == "SI":
-                    scaled_inputs()
-
-        items(PLAN["main0" if t == 0 else "main"])
-
-        tt(A("hi"), A("pL", 0, L), A("thp"), Op.is_ge)
-        for r in range(16):
-            mm(A("pC", 0, 16), E("WE", r), A("hi", r, L, 16), False, r == 15)
-        items(PLAN["tail"])
-
-        l1r = A("L1R", t * 16, (t + 1) * 16)
-
-        def clear():
-            cp(IND(A("M"), l1r), A("MR", V, VX))
-
-        def merge():
-            tt(lanesM, lanesM, A("back"), Op.max)
-
-        if t < 3:
-            su_list(t + 1, 0, L)
-        act(A("MR", t * VX + q, t * VX + V, 4), A("FR", t * L, (t + 1) * L))
-        act(A("back"), IND(A("MR", t * VX, (t + 1) * VX), l1), -4.0)
-        early = PLAN["m_early"]
-        if early >= 1:
-            clear()
-        tt(A("tt1"), A("pD", 0, L), A("hi"), Op.mult)
-        mm(A("pZ", 0, L), MAT(0), A("tt1"), False, True)
-        if early >= 2:
-            merge()
-        ch = A("CH", t * L, (t + 1) * L)
-        if last:
-            ts(A("t2"), A("pZ", 0, L), float(W), Op.is_ge, -float(W), Op.mult)
-            tt(A("t3"), A("pZ", 0, L), A("t2"), Op.add)
-            cp(ch, A("t3"))
-        else:
-            cp(ch, A("pZ", 0, L))
-        send(ch, dest(t), A("CHR", t * L, (t + 1) * L), "a2%d" % t, "l2")
-        if early < 1:
-            clear()
-        if early < 2:
-            merge()
-        if not last:
-            send_levels(t + 1)
-            items(PLAN["window"], t + 1)
-            cp(IND(A("P"), l1r), A("CHR", t * L, (t + 1) * L))
-        else:
-            store("s", T.ymk[:], A("M", 0, V), "d_om")
-            for k, bank in enumerate(("pS", "pO")):
-                act(A("gm", 512 * k, 512 * k + 512), A("P", 512 * k, 512 * k + 512), 0.5 - W, 1.0, Fn.Sign)
-                act(A(bank), A("gm", 512 * k, 512 * k + 512), -W / 2.0, -W / 2.0)
-            for k, bank in enumerate(("pS", "pO")):
-                tt(A("P", 512 * k, 512 * k + 512), A(bank), A("P", 512 * k, 512 * k + 512), Op.add)
-            cp(IND(A("P"), l1r), A("CHR", t * L, (t + 1) * L))
-            store("s", T.ypl[:], A("P", 0, V), "d_op")
+        run(PLAN["first" if t == 0 else "last" if t == RO - 1 else "mid"], t)
 
     number = {}
     count = {q: 0 for q in CNT}

import math
from concourse.mybir import AluOpType as Op, ActivationFunctionType as Fn

W, V, L, RO = 3840, 1024, 256, 6
WX = 5120
VX = V + L
BF, F32, I32, U16 = "bfloat16", "float32", "int32", "uint16"
BITS, LOW = 14, -84
ZERO, DOWN, HIGH = 2.0 ** LOW, 2.0 ** (-4 * BITS), 2.0 ** 25
HALF_TOP = 2.0 ** ((15 * BITS + LOW) // 2)
LN2 = math.log(2.0)


def _sb(n, d):
    return ("sbuf", [128, n], d)


SCRATCH = {
    "X": _sb(WX, BF), "ST": _sb(WX, BF), "P": _sb(VX, F32), "PL": _sb(V, I32), "M": _sb(VX, BF),
    "SU": _sb(V, I32), "SL": _sb(V, U16), "HP": _sb(64, I32), "CP": _sb(4, I32), "TH": _sb(8, I32),
    "hc": _sb(64, F32), "hd": _sb(64, F32), "ht": _sb(64, F32), "hs": _sb(64, F32),
    "cpf": _sb(4, F32), "thf": _sb(8, F32), "rem": _sb(4, F32),
    "xk": _sb(4096, BF), "sk": _sb(4096, BF), "skT": _sb(4096, BF), "gm": _sb(4096, BF), "y": _sb(4096, BF),
    "offs": _sb(L, U16), "SS": _sb(3 * L, BF), "ov": _sb(L, BF), "hi": _sb(L, BF), "f15": _sb(L, BF),
    "R": _sb(L, BF), "tt1": _sb(L, BF), "t2": _sb(L, F32), "t3": _sb(L, F32), "zero": _sb(L, BF), "low": _sb(L, BF),
    "MK": _sb(V, BF), "MO": _sb(VX, BF), "bk": _sb(L, BF),
    "dc": _sb(1536, BF), "dh": _sb(1536, BF), "dw": _sb(1536, BF), "dr": _sb(1536, BF),
    "ui": _sb(32, I32), "uw": _sb(32, I32), "jm": _sb(16, F32), "ja": _sb(16, F32), "jl": _sb(16, U16), "jb": _sb(16, F32),
    "li": _sb(16, F32), "tm": _sb(16, F32), "ob": _sb(16, BF), "af": _sb(4, F32), "ak": _sb(8, BF), "dl": _sb(32, BF),
    "NEW": _sb((RO + 1) * L, BF), "L1": _sb(RO * 16, U16), "CH": _sb(RO * L, U16),
    "MR": _sb(RO * VX, BF), "FR": _sb(RO * L, BF), "L1R": _sb(RO * 16, U16), "CHR": _sb(RO * L, U16),
    "ip": _sb(4, I32), "KI": _sb(8, I32), "KF": _sb(8, F32), "KD": _sb(8, F32),
    "ion": _sb(144, BF), "iog": _sb(128, BF), "io16": _sb(16, F32), "IF": _sb(128, F32), "BH": _sb(128, F32),
    "WE": _sb(144, BF), "WN": _sb(144, BF), "WW": _sb(144, BF), "MAT": _sb(13 * 128, BF),
}
for _bank in ("pS", "pA", "pL", "pC", "pG", "pU", "pZ", "pD"):
    SCRATCH[_bank] = ("psum", [128, 512], F32)
LOADS = ["d_mk", "d_su", "d_su2", "d_pl", "d_x", "d_s", "d_xe", "d_se", "d_hp", "d_cp", "d_th", "d_om", "d_op"]
SEMAPHORES = (["cv", "ca", "ct", "cg"] + LOADS + ["lm", "ln", "l1", "l2"]
              + ["%s%d" % (k, t) for k in ("am", "an", "a1", "a2") for t in range(RO)])

PLAN = {
    "first": "ML L:0-128 mv:64-128 SC SD ma:0-64 L:128-256 ma:128-192 c:64-128 IC PC F:0-128 xa:64-96 F:128-256 xa:0-32 xa:128-160 xa:192-224 xv:96-128 xv:32-64 S:0-128 xv:224-256 c:0-64 xv:160-192 c:128-192 sv:192-224 ma:192-256 c:192-256 S:128-256 lv O D0 sa:96-128 na sa:224-256 Vm p y:0-2 y:2-4 y:4-6 ev sa:32-64 U y:6-8 t:224-256 y:8-10 y:10-12 y:12-14 sa:64-96 t:192-224 t:64-128 u:0 u:9 u:1 u:2 y:14-16 h0 u:3 h u:4 u:5 u:6 hj u:7 fw u:8 hm at nw fr sa:0-32 t:0-64 Z:0-128 sa:128-192 t:128-192 Z:128-256 R:0-128 R:128-256 Rm tm l1 L+ tt1 ch pa ca ob cl bo mg ML+ oc ma+:0-64 ma+:128-192 mv+:64-128 ps",
    "mid": "D0 F:0-128 xa:0-32 xa:64-96 F:128-256 xa:128-160 xa:192-224 xv:96-128 xv:32-64 S:0-128 xv:160-192 xv:224-256 S:128-256 c:64-128 sv:192-224 c:0-64 t:192-224 O lv Vm sa:96-128 ma:224-256 sa:224-256 y:0-2 y:2-4 c:128-192 y:4-6 ma:192-224 na ea y:6-8 y:8-10 U c:192-256 y:10-12 p t:224-256 y:12-14 u:0 y:14-16 u:1 u:9 sa:64-96 u:2 h t:64-128 u:3 at h0 hj u:5 hm u:4 u:7 fw u:6 nw fr sa:0-32 u:8 sa:32-64 t:0-64 Z:0-128 sa:128-192 t:128-192 tm l1 R:0-128 ca R:128-256 Z:128-256 Rm tt1 L+ ch pa bo ob cl mg ma+:0-64 mv+:64-128 ps oc ML+ ma+:128-192",
    "last": "F:0-128 F:128-256 xv:96-128 xv:32-64 xa:64-96 xa:0-32 S:0-128 xv:160-192 xv:224-256 sv:192-224 c:0-64 c:64-128 t:192-224 xa:192-224 xa:128-160 S:128-256 D0 O lv Vm na ma:192-224 ma:224-256 sa:224-256 y:0-2 y:2-4 ea U y:4-6 c:128-192 y:6-8 c:192-256 y:8-10 u:9 u:0 p y:10-12 y:12-14 u:1 y:14-16 u:5 h u:7 t:224-256 u:8 fw hj at h0 nw hm fr sa:0-32 sa:64-96 sa:32-64 sa:96-128 t:64-128 t:0-64 Z:0-128 sa:128-192 t:128-192 Z:128-256 u:2 u:3 u:4 u:6 tm l1 R:0-128 R:128-256 pa wr:512-1024 bo Rm tt1 ch ws:512-1024 ca cl wr:0-512 ws:0-512 mg om ps op",
}
PLAN = {
    "first": "L:0-128 EN ML ma:0-64 mv:64-128 L:128-256 G0 G:0-128 F:128-256 mv:192-256 IC F:0-128 nv sp:1-3 ma:128-192 G:128-256 SC xa:96-128 xv:64-96 S:64-128 xa:0-32 xv:32-64 S:0-64 xa:128-160 xv:160-192 S:128-192 xv:224-256 PC xa:192-224 S:192-256 O y:0-2 y:2-4 sa:128-160 SD la Vm sa:0-64 y:4-6 ea sa:160-224 y:6-8 y:8-10 y:10-12 y:12-14 y:14-16 t:0-32 U sv:96-128 fv t:128-160 t:96-128 D0 u:0 u:9 h0 new fr G0+ u:1 hi hm u:2 u:5 u:3 u:7 u:4 sa:64-96 t:64-96 u:6 t:160-192 sa:224-256 tm u:8 l1 sp:0-1 t:32-64 R:0-128 at Z:0-128 t:192-224 t:224-256 R:128-256 Z:128-256 Rm cm tt1 L+ ch sp:6-8 cl pa ob oc bo mg mv+:128-192 G+:128-192 sp:3-6 ma+:0-64 G+:0-64 ma+:64-128 G+:64-128 sp:8-9 ps ML+ nv+",
    "mid": "D0 F:0-128 xa:0-32 F:128-256 xv:32-64 xv:96-128 xa:64-96 S:0-64 S:64-128 xv:160-192 xa:128-160 S:128-192 xa:192-224 xv:224-256 S:192-256 mv:192-256 G:192-256 O y:0-2 sa:0-64 la Vm y:2-4 y:4-6 t:0-32 y:6-8 sa:64-96 t:64-96 y:8-10 y:10-12 y:12-14 y:14-16 t:32-64 sa:128-160 ea sa:96-128 U sa:160-224 fv t:96-128 sa:224-256 u:0 u:9 u:1 new fr u:2 u:5 hi u:3 at t:128-160 u:4 u:7 u:6 t:160-192 h0 hm tm u:8 l1 Z:0-128 G0+ R:0-128 t:192-224 t:224-256 Z:128-256 R:128-256 Rm ob L+ cm tt1 oc ch pa cl bo mg mv+:128-192 G+:128-192 ma+:0-64 G+:0-64 ma+:64-128 ps nv+ ML+ G+:64-128",
    "last": "F:0-128 F:128-256 xv:32-64 xa:0-32 S:0-64 xa:64-96 xv:96-128 S:64-128 xv:160-192 xa:128-160 S:128-192 xa:192-224 xv:224-256 S:192-256 mv:192-256 G:192-256 O y:0-2 lv sa:96-128 sa:128-160 sa:64-96 sa:0-64 y:2-4 Vm y:4-6 y:6-8 y:8-10 y:10-12 y:12-14 t:64-96 y:14-16 t:32-64 t:96-128 t:128-160 ea U fv t:0-32 D0 at Z:0-128 sa:224-256 t:224-256 u:0 u:1 u:9 h0 u:5 new fr u:7 sa:160-224 t:192-224 u:8 t:160-192 Z:128-256 R:0-128 u:2 hi u:3 wv:0-512 u:4 wv:512-1024 u:6 dc:0-512 hm tm R:128-256 Rm tt1 l1 dc:512-1024 ch ws:512-1024 ws:0-512 da:0-512 dr:0-512 pa da:512-1024 bo dc:1024-1536 dr:512-1024 ps op da:1024-1536 dr:1024-1536 cl mg om",
}
TRACE = []


def rank_program(g, core, T, topo):
    rank = T.rank_of(core)
    if rank is None:
        return
    N = len(T.cores)
    Q = {"v": g.vector, "a": g.scalar, "t": g.tensor, "g": g, "s": g.sync}
    CNT = {"v": "cv", "a": "ca", "t": "ct", "g": "cg"}
    ops = []
    recs = {}
    seen = {q: {} for q in Q}
    totals = {}

    def A(name, lo=0, hi=None, step=1):
        hi = SCRATCH[name][1][1] if hi is None else hi
        ap = T[name][:, lo:hi] if step == 1 else T[name][:, lo:hi:step]
        return (ap, name, lo, hi, step)

    def IND(win, off):
        return (win[0].indirect(off[0]), win[1], win[2], win[3], 2, off)

    def note(a, writes, token, q):
        rl = recs.setdefault(a[1], [])
        if writes and a[4] == 1 and SCRATCH[a[1]][0] != "psum":
            rl[:] = [r for r in rl if not (a[2] <= r[0] and r[1] <= a[3])]
        rl.append((a[2], a[3], writes, token, q))

    def emit(q, call, reads, writes, own=None):
        reads = list(reads) + [a[5] for a in list(reads) + list(writes) if len(a) > 5]
        TRACE.append((q, [a[1:4] for a in reads], [a[1:4] for a in writes]))
        need = {}
        for a, wr in [(a, False) for a in reads] + [(a, True) for a in writes]:
            psum = SCRATCH[a[1]][0] == "psum"
            for lo, hi, w, tok, rq in recs.get(a[1], []):
                if psum and rq != q:
                    hit = True
                elif psum and q == "t":
                    hit = False
                else:
                    hit = (w or wr) and lo < a[3] and a[2] < hi
                if hit and tok[1] > need.get(tok[0], -1):
                    need[tok[0]] = tok[1]
        waits = []
        for s, v in need.items():
            if seen[q].get(s, -1) < v:
                seen[q][s] = v
                waits.append((s, v))
                if s in CNT:
                    ops[v][3] = True
        token = (q, len(ops)) if own is None else own
        ops.append([q, call, waits, False, own])
        for a in reads:
            note(a, False, token, q if own is None else "dma")
        for a in writes:
            note(a, True, token, q if own is None else "dma")

    def col(s):
        return [s] if isinstance(s, tuple) else []

    def val(s):
        return s[0] if isinstance(s, tuple) else s

    def cp(out, a):
        emit("v", lambda: g.vector.tensor_copy(out[0], a[0]), [a], [out])

    def tt(out, a, b, op):
        emit("v", lambda: g.vector.tensor_tensor(out[0], a[0], b[0], op), [a, b], [out])

    def ts(out, a, s1, op0, s2=None, op1=None):
        if op1 is None:
            emit("v", lambda: g.vector.tensor_scalar(out[0], a[0], val(s1), None, op0), [a] + col(s1), [out])
        else:
            emit("v", lambda: g.vector.tensor_scalar(out[0], a[0], val(s1), val(s2), op0, op1), [a] + col(s1) + col(s2), [out])

    def scan(out, d0, d1, op0, op1):
        emit("v", lambda: g.vector.tensor_tensor_scan(out[0], d0[0], d1[0], 0.0, op0, op1), [d0, d1], [out])

    def fill(out, c):
        emit("v", lambda: g.vector.memset(out[0], c), [], [out])

    def act(out, a, bias=None, scale=1.0, fn=Fn.Identity, acc=None):
        if bias is None:
            emit("a", lambda: g.scalar.activation(out[0], a[0], Fn.Copy), [a], [out])
        elif acc is None:
            emit("a", lambda: g.scalar.activation(out[0], a[0], fn, bias=val(bias), scale=val(scale)),
                 [a] + col(bias) + col(scale), [out])
        else:
            emit("a", lambda: g.scalar.activation(out[0], a[0], fn, bias=val(bias), scale=scale, accum_out=acc[0]),
                 [a] + col(bias), [out, acc])

    def move(e, out, a, scale=1.0, bias=0.0):
        if scale == 1.0 and bias == 0.0:
            (act if e == "a" else cp)(out, a)
        elif e == "a":
            act(out, a, bias, scale)
        else:
            ts(out, a, scale, Op.mult, bias, Op.add)

    def mm(out, lhs, rhs, start, stop):
        emit("t", lambda: g.tensor.matmul(out[0], lhs[0], rhs[0], start, stop), [lhs, rhs], [out])

    def iota(out, pattern, mult, small=True):
        if small:
            emit("g", lambda: g.iota(out[0], pattern, 0, mult, allow_small_or_imprecise_dtypes=True), [], [out])
        else:
            emit("g", lambda: g.iota(out[0], pattern, 0, mult), [], [out])

    def load(q, out, src, sem):
        totals[sem] = 16
        emit(q, lambda: Q[q].dma_start(out[0], src).then_inc(T.sem[sem], 16), [], [out], own=(sem, 16))

    def store(q, dst, a, sem):
        totals[sem] = 16
        emit(q, lambda: Q[q].dma_start(dst, a[0]).then_inc(T.sem[sem], 16), [a], [], own=(sem, 16))

    def send(a, to, land, rsem, lsem, after=()):
        dst = T.cores[to]
        rid, pid, se = topo.addr(dst)
        totals[lsem] = totals.get(lsem, 0) + len(topo.engines(core, dst))
        emit("g", lambda: g.remote_dma(land[0], a[0], T.sem[rsem], T.sem[lsem], pid, rid, topo.mask(core, dst)),
             [a] + list(after), [], own=(lsem, totals[lsem]))

    def expect(land, frm, rsem):
        totals[rsem] = len(topo.engines(T.cores[frm], core))
        note(land, True, (rsem, totals[rsem]), "dma")

    def dest(t):
        return (rank + 1 + t % (N - 1)) % N

    def source(t):
        return (rank - 1 - t % (N - 1)) % N

    for t in range(RO):
        expect(A("MR", t * VX, t * VX + V), dest(t), "am%d" % t)
        expect(A("FR", t * L, (t + 1) * L), dest(t), "an%d" % t)
        expect(A("L1R", t * 16, (t + 1) * 16), source(t), "a1%d" % t)
        expect(A("CHR", t * L, (t + 1) * L), source(t), "a2%d" % t)

    load("s", A("MK"), T.mk[:], "d_mk")
    load("s", A("SU", 0, V // 2), T.su[:, 0:V // 2], "d_su")
    load("s", A("SU", V // 2, V), T.su[:, V // 2:V], "d_su2")
    load("s", A("PL"), T.pl[:], "d_pl")
    load("s", A("X", 0, W), T.xf[:], "d_x")
    load("s", A("ST", 0, W), T.stp[:], "d_s")
    load("a", A("HP"), T.hp[:], "d_hp")
    load("a", A("TH", 0, RO), T.th[:], "d_th")
    load("a", A("CP", 0, 1), T.cp[:], "d_cp")
    load("s", A("X", W, WX), T.xf[:, 0:WX - W], "d_xe")
    load("s", A("ST", W, WX), T.stp[:, 0:WX - W], "d_se")

    iota(A("ip", 0, 1), [[0, 1]], 1, False)
    iota(A("ion"), [[1, 144]], 0)
    iota(A("iog"), [[1, 8], [0, 16]], 0)
    iota(A("io16"), [[1, 16]], 0)
    ip = A("ip", 0, 1)

    def MAT(k):
        return A("MAT", 128 * k, 128 * (k + 1))

    ONE, NEG, NIL, FALL, TOP = [MAT(k) for k in (0, 1, 10, 11, 12)]
    SORT = [[2, 5], [4, 3]]

    def encode(out, a):
        act(out, a, LOW * LN2, BITS * LN2, Fn.Exp)

    fill(A("zero"), 0.0)
    encode(A("M", V, VX), A("zero"))
    for k, (c, op) in enumerate([(127, Op.bitwise_and), (15, Op.bitwise_and), (112, Op.bitwise_and), (16, Op.bitwise_and),
                                 (4, Op.arith_shift_right)]):
        ts(A("KI", k, k + 1), ip, c, op)
    cp(A("KF", 0, 5), A("KI", 0, 5))
    kp, kr, kg, kh, kgi = [A("KF", k, k + 1) for k in range(5)]
    gE, hs, psw, wt, m0, m1 = [A("KD", k, k + 1) for k in range(6)]
    ts(gE, kg, 15.0, Op.add)
    ts(hs, kh, -2.0, Op.mult, 16.0, Op.add)
    ts(wt, kr, 2.0, Op.mult, 1.0, Op.add)
    ts(m1, kh, 1.0 / 16, Op.mult)
    ts(m0, kh, -1.0 / 16, Op.mult, 1.0, Op.add)
    ts(psw, hs, kp, Op.add)
    i128 = A("ion", 0, 128)
    ts(ONE, i128, kp, Op.is_equal)
    ts(A("WE"), A("ion"), gE, Op.is_equal)
    for k, (tg, mk) in enumerate([(kp, m0), (kp, m1), (psw, m1), (psw, m0)]):
        ts(MAT(2 + k), i128, tg, Op.is_equal, mk, Op.mult)
    ts(A("BH"), A("iog"), kgi, Op.is_equal, 0.5, Op.mult)
    ts(A("li"), A("io16"), 16.0, Op.mult, kr, Op.add)
    ts(A("dl", 0, 16), A("li"), -1.0 / 2048, Op.mult)
    ts(A("jb"), A("li"), 16.0, Op.mult)
    fill(A("ht"), 0.0)
    ts(FALL, i128, kp, Op.is_equal, DOWN, Op.mult)
    fill(NIL, 0.0)

    def spare(k):
        if k < RO:
            act(A("MR", k * VX + V, (k + 1) * VX), A("M", V, VX))
        else:
            act(A(("low", "P", "MO")[k - RO], *((0, L), (V, VX), (V, VX))[k - RO]), A("M", V, VX))

    def scaled_constants():
        act(NEG, ONE, 0.0, -1.0)
        act(A("IF"), ONE)
        act(A("WW"), A("WE"), 0.0, wt)
        act(A("WN"), A("WE"), 0.0, -1.0)
        act(TOP, ONE, 0.0, HALF_TOP)

    def step_constants():
        for k in range(4):
            act(MAT(6 + k), MAT(2 + k), 0.0, -1.0)

    def input_constants():
        ts(A("hc"), A("HP"), -1.0 / 2048, Op.mult, 0.5, Op.add)
        cp(A("thf", 0, RO), A("TH", 0, RO))
        ts(A("cpf", 0, 1), A("CP", 0, 1), 1216.0, Op.add)
        fill(A("rem", 0, 1), -1216.0)
        for k in range(3):
            tt(A("hd", k, 64, 4), A("hc", 48 - 16 * k, 64 - 16 * k), A("hc", 32 - 16 * k, 48 - 16 * k), Op.subtract)
        ts(A("hd", 3, 64, 4), A("hc", 0, 16), 256.0, Op.add)

    def E(name, r):
        return A(name, 15 - r, 143 - r)

    small = [
        lambda: cp(A("ui"), A("pU", 0, 32)),
        lambda: ts(A("uw"), A("ui"), 63, Op.bitwise_and),
        lambda: ts(A("ht", 1, 64, 4), A("uw", 16, 32), 48.0, Op.is_ge),
        lambda: ts(A("ht", 2, 64, 4), A("uw", 16, 32), 32.0, Op.is_ge),
        lambda: ts(A("ht", 3, 64, 4), A("uw", 16, 32), 16.0, Op.is_ge),
        lambda: ts(A("jm"), A("uw", 0, 16), 0.25, Op.mult, 1.0, Op.max),
        lambda: scan(A("hs"), A("ht"), A("hd"), Op.mult, Op.add),
        lambda: tt(A("ja"), A("jm"), A("jb"), Op.add),
        lambda: cp(A("jl"), A("ja")),
        lambda: cp(A("dl", 16, 32), A("pU", 32, 48)),
    ]

    def step(n, t, lo, hi):
        q = t % 4
        wx = W if t == 0 else WX
        last = t == RO - 1
        lanesM, lanesP, lanesO = A("M", q, V, 4), A("P", q, V, 4), A("MO", q, V, 4)
        back = A("NEW", RO * L, (RO + 1) * L)
        new, l1, ch = A("NEW", t * L, (t + 1) * L), A("L1", t * 16, (t + 1) * 16), A("CH", t * L, (t + 1) * L)
        l1r = A("L1R", t * 16, (t + 1) * 16)
        th = A("thf", t, t + 1)
        wide = (16 * lo, 16 * hi)
        if n == "F":
            cp(A("offs", lo, hi), A("P" if t else "PL", 4 * lo + q, 4 * hi, 4))
        elif n == "L":
            if t < 4:
                cp(A("SL", q * L + lo, q * L + hi), A("SU", 4 * lo + q, 4 * hi, 4))
        elif n in ("xa", "xv"):
            move(n[1], A("xk", *wide), IND(A("X", 0, wx), A("offs", lo, hi)), -1.0)
        elif n in ("sa", "sv"):
            move(n[1], A("sk", *wide), IND(A("ST", 0, wx), A("offs", lo, hi)))
        elif n in ("ma", "mv"):
            move(n[1], A("gm", *wide), IND(A("M", 0, V), A("SL", q * L + lo, q * L + hi)))
        elif n == "G0":
            mm(A("pG", 0, L), NIL, A("zero"), True, False)
        elif n == "G":
            for k in range(16):
                mm(A("pG", lo, hi), FALL, A("gm", 16 * lo + k, 16 * hi, 16), False, False)
        elif n == "nv":
            ts(A("SS", 2 * L, 3 * L), lanesM, HIGH, Op.is_lt)
        elif n == "S":
            for a in range(16):
                mm(A("pS", lo, hi), NEG, A("xk", 16 * lo + a, 16 * hi, 16), a == 0, a == 15)
        elif n in ("la", "lv"):
            move(n[1], A("SS", L, 2 * L), A("pS", 0, L))
        elif n == "O":
            ts(A("ov"), A("pS", 0, L), A("cpf", 0, 1), Op.subtract, A("rem", 0, 1), Op.is_gt)
        elif n == "y":
            for a in range(lo, hi):
                ya = A("y", a * L, (a + 1) * L)
                scan(ya, A("ov"), A("xk", a, 16 * L, 16), Op.max, Op.mult)
                mm(A("pL", 0, L), E("WN", a), ya, a == 0, a == 15)
        elif n == "fv":
            ts(A("f15"), A("pL", 0, L), th, Op.is_ge, HALF_TOP, Op.mult)
            mm(A("pG", 0, L), TOP, A("f15"), False, True)
        elif n == "new":
            tt(new, A("pG", 0, L), lanesM, Op.max)
        elif n == "hi":
            ts(A("hi"), new, HIGH, Op.is_ge)
        elif n == "fr":
            send(new, source(t), A("FR", t * L, (t + 1) * L), "an%d" % t, "ln")
        elif n in ("cm", "ca"):
            move("v" if n == "cm" else "a", lanesM, new)
        elif n == "Vm":
            for h in range(2):
                for x in range(2):
                    mm(A("pS", L + h, 2 * L, 2), MAT(SORT[h][x]), A("SS", L + x, 2 * L, 2), x == 0, x == 1)
        elif n in ("ea", "ev"):
            move(n[1], A("SS", 0, L), A("pS", L, 2 * L), 4.0)
        elif n == "U":
            for r in range(16):
                mm(A("pU", 0, 48), E("WW", r), A("SS", r, 3 * L, 16), r == 0, r == 15)
        elif n == "u":
            small[lo]()
        elif n == "h0":
            mm(A("pC", 0, 16), ONE, A("dl", 0, 16), True, False)
            mm(A("pC", 0, 16), ONE, A("dl", 16, 32), False, False)
        elif n == "hm":
            for r in range(16):
                mm(A("pC", 0, 16), E("WW", r), A("hi", r, L, 16), False, r == 15)
        elif n == "tm":
            tt(A("tm"), A("pC", 0, 16), A("hs", 3, 64, 4), Op.min)
        elif n == "l1":
            ts(l1, A("tm"), -2048.0, Op.mult, float(V + 256 * 2048), Op.add)
            send(l1, dest(t), l1r, "a1%d" % t, "l1")
        elif n == "ob":
            act(A("ob"), A("tm"), -256.0 - 1.0 / 4096, 1.0, Fn.Sign, A("af", 0, 1))
            mm(A("pA", 0, 1), A("BH"), A("af", 0, 1), True, True)
            act(A("ak", 0, 1), A("pA", 0, 1), 151.5625, 0.125)
        elif n == "oc":
            ts(A("rem", 0, 1), A("ak", 0, 1), -8.0, Op.mult, A("pA", 0, 1), Op.add)
        elif n == "t":
            o, i = A("skT", *wide), A("sk", *wide)
            emit("v", lambda: g.vector.transpose(o[0], i[0]), [i], [o])
        elif n == "D0":
            mm(A("pD", 0, L), NIL, A("zero"), True, False)
        elif n == "at":
            mm(A("pZ", 0, L), A("IF"), lanesP, True, False)
        elif n == "Z":
            for bank, m in (("pD", 4), ("pZ", 0)):
                for x in range(2):
                    for h in range(2):
                        mm(A(bank, lo + x, hi, 2), MAT(m + SORT[x][h]), A("skT", 16 * lo + 16 * h, 16 * hi, 32), False, False)
        elif n == "R":
            act(A("R", lo, hi), IND(A("skT", 0, 16 * hi), A("jl", lo // 16, hi // 16)))
        elif n == "Rm":
            for x in range(2):
                for h in range(2):
                    mm(A("pD", x, L, 2), MAT(SORT[x][h]), A("R", h, L, 2), False, x + h == 2)
        elif n == "tt1":
            tt(A("tt1"), A("hi"), A("pD", 0, L), Op.mult)
            mm(A("pZ", 0, L), ONE, A("tt1"), False, True)
        elif n == "ch":
            if t == RO - 1:
                ts(A("t2"), A("pZ", 0, L), float(W), Op.is_ge, -float(W), Op.mult)
                tt(A("t3"), A("pZ", 0, L), A("t2"), Op.add)
                cp(ch, A("t3"))
            else:
                cp(ch, A("pZ", 0, L))
            send(ch, dest(t), A("CHR", t * L, (t + 1) * L), "a2%d" % t, "l2")
        elif n in ("pv", "pa"):
            move(n[1], A("MR", t * VX + q, t * VX + V, 4), A("FR", t * L, (t + 1) * L))
        elif n == "bo":
            move("a", back, IND(A("MR", t * VX, (t + 1) * VX), l1), DOWN)
        elif n == "cl":
            cp(IND(A("MO" if last else "M"), l1r), A("zero" if last else "low"))
        elif n == "mg":
            if last:
                tt(lanesO, lanesO, A("bk"), Op.max)
            else:
                tt(lanesM, lanesM, back, Op.max)
        elif n == "ML":
            after = [A("CHR", (t - 1) * L, t * L)] if t else []
            send(A("M", 0, V), source(t), A("MR", t * VX, t * VX + V), "am%d" % t, "lm", after)
        elif n == "ps":
            cp(IND(A("P"), l1r), A("CHR", t * L, (t + 1) * L))
        elif n == "PC":
            cp(A("P", 0, V), A("PL"))
        elif n == "sp":
            for k in range(lo, hi):
                spare(k)
        elif n == "EN":
            encode(A("M", 0, V), A("MK"))
        elif n in ("dc", "da", "dr"):
            coded = A("M", lo, hi) if lo < V else A("NEW", t * L, (t + 2) * L)
            bank = A(("pS", "pA", "pU")[lo // 512])
            if n == "dc":
                ts(A("dc", lo, hi), coded, HIGH, Op.min, ZERO, Op.max)
            elif n == "da":
                act(A("dh", lo, hi), coded, 2.0 ** -50, 2.0 ** -75, Fn.Ln)
                act(A("dw", lo, hi), A("dc", lo, hi), 0.0, 2.0 ** 30, Fn.Ln)
                mm(bank, ONE, A("dh", lo, hi), True, False)
                mm(bank, ONE, A("dw", lo, hi), False, True)
            else:
                ts(A("dr", lo, hi), bank, 1.0 / (BITS * LN2), Op.mult, 136.0 + (20 - LOW - 6.2) / BITS, Op.add)
                if lo < V:
                    ts(A("MO", lo, hi), A("dr", lo, hi), -136.0, Op.add)
                else:
                    ts(lanesO, A("dr", V, V + L), -136.0, Op.add)
                    ts(A("bk"), A("dr", V + L, V + 2 * L), -136.0, Op.add)
        elif n == "wv":
            ts(A(("pL", "pG")[lo // 512]), A("P", lo, hi), float(W), Op.is_ge, -float(W), Op.mult)
        elif n == "ws":
            tt(A("P", lo, hi), A(("pL", "pG")[lo // 512]), A("P", lo, hi), Op.add)
        elif n == "om":
            store("s", T.ymk[:], A("MO", 0, V), "d_om")
        elif n == "op":
            store("s", T.ypl[:], A("P", 0, V), "d_op")
        else:
            {"SC": scaled_constants, "SD": step_constants, "IC": input_constants}[n]()

    def run(script, t):
        for word in script.split():
            TRACE.append(word)
            n, _c, span = word.partition(":")
            lo, hi = ([int(v) for v in span.split("-")] + [0])[:2] if span else (0, L)
            step(n.rstrip("+"), t + n.endswith("+"), lo, hi)

    for t in range(RO):
        run(PLAN["first" if t == 0 else "last" if t == RO - 1 else "mid"], t)

    number = {}
    count = {q: 0 for q in CNT}
    for k, (q, call, waits, marked, own) in enumerate(ops):
        if marked:
            count[q] += 1
            number[k] = count[q]
    for k, (q, call, waits, marked, own) in enumerate(ops):
        for s, v in waits:
            if s in CNT:
                Q[q].wait_ge(T.sem[CNT[s]], number[v])
            else:
                Q[q].wait_ge(T.sem[s], v)
        ins = call()
        if marked:
            ins.then_inc(T.sem[CNT[q]], 1)
    for s, v in totals.items():
        g.wait_ge(T.sem[s], v)
